import numpy as np
import ml_dtypes


def mxq(x, axis, fmt="e4m3"):
    dtype, down = {"e4m3": (ml_dtypes.float8_e4m3fn, 7), "e5m2": (ml_dtypes.float8_e5m2, 14)}[fmt]
    v = np.moveaxis(np.asarray(x, np.float32).astype(ml_dtypes.bfloat16).astype(np.float64), axis, -1)
    blocks = v.reshape(v.shape[:-1] + (-1, 32))
    amax = np.abs(blocks).max(-1, keepdims=True)
    byte = np.maximum(np.where(amax > 0, np.frexp(amax)[1] - 1 + 127, 0) - down, 1)
    scale = np.exp2(byte - 127.0)
    codes = (blocks / scale).astype(np.float32).astype(dtype).astype(np.float64)
    return np.moveaxis((codes * scale).reshape(v.shape), -1, axis)


WIDE = False


def mx_kscale(k):
    if not WIDE:
        return np.ones(k)
    levels = np.array([10, -10, 5, -5, 0])
    if k % 512:
        return np.exp2(np.random.permutation(np.resize(levels, k // 32))).repeat(32)
    a = np.empty((k // 512, 16))
    for p in range(k // 512):
        a[p, :8] = np.random.permutation(np.resize(levels, 8))
        for g in range(8):
            far = levels[np.abs(levels - a[p, g]) >= 10]
            a[p, g + 8] = far[np.random.randint(len(far))]
    return np.exp2(a.ravel()).repeat(32)


def f64(x):
    return np.asarray(x).astype(np.float64)


def striped(idx):
    return np.tile(idx.reshape(-1, 16).T, (8, 1)).astype(np.uint16)


def unstriped(offs):
    return offs[:16].T.reshape(-1).astype(np.int64)


def pack_weight(w):
    k, n = w.shape
    w = f64(np.asarray(w, np.float32).astype(ml_dtypes.bfloat16)).reshape(k // 32, 32, n)
    amax = np.abs(w).max(1)
    byte = np.clip(np.where(amax > 0, np.frexp(amax)[1] - 1 + 127 - 7, 1), 1, 254)
    scaled = (w * np.exp2(127.0 - byte)[:, None, :]).reshape(k, n).astype(np.float32)
    words = np.ascontiguousarray(scaled.reshape(k // 512, 128, 4, n).transpose(0, 1, 3, 2)).astype(ml_dtypes.float8_e4m3fn).view(np.uint8)
    return words, np.ascontiguousarray(byte.astype(np.uint8).reshape(k // 512, 16, n))


def unpack_weight(words, scales):
    g, p, n, _ = words.shape
    vals = np.ascontiguousarray(words).view(ml_dtypes.float8_e4m3fn).astype(np.float64) * np.repeat(np.exp2(scales.astype(np.float64) - 127.0), 8, axis=1)[..., None]
    return vals.transpose(0, 1, 3, 2).reshape(g * 512, n)


def planes(y):
    n, m = y.shape
    v = y.astype(np.float32).astype(ml_dtypes.bfloat16).astype(np.float64).reshape(n // 32, 32, m)
    top = np.abs(v).max(1)
    byte = np.clip(np.where(top > 0, np.frexp(top)[1] - 1 + 127 - 7, 1), 1, 254)
    codes = (v * np.exp2(127.0 - byte)[:, None, :]).reshape(n, m).astype(np.float32).astype(ml_dtypes.float8_e4m3fn).view(np.uint8)
    words = codes.reshape(n // 512, 128, 4, m).transpose(0, 1, 3, 2)
    return np.ascontiguousarray(words), np.ascontiguousarray(byte.astype(np.uint8).reshape(n // 512, 16, m))


def sigmoid(v):
    return 1.0 / (1.0 + np.exp(-np.maximum(v, -700.0)))


K, T, S, V, N, D = 1024, 2048, 512, 256, 512, 2
P = 2 ** 7


def setup_inputs():
    n = np.random.standard_normal
    s = mx_kscale(K)[:, None]
    near = np.random.permutation(S)
    packed_xT = pack_weight(n((K, T)) * s)
    return {
        "x_words": packed_xT[0],
        "x_scales": packed_xT[1],
        "w1": (n((K, N)) / np.sqrt(K) / s).astype(np.float32),
        "w2": (n((K, N)) / np.sqrt(K) / s).astype(np.float32),
        "w3": (n((K, N)) / np.sqrt(K) / s).astype(np.float32),
        "pos": (np.tile(n((D, 1, V)) * 0.7, (1, P, 1))).astype(np.float32),
        "offs": striped(np.random.permutation(T)[:S]),
        "pos1": striped(near[:V]),
        "pos2": striped(near[V:]),
        "own": striped(np.random.permutation(S)[:V]),
    }


def reference(x_words, x_scales, w1, w2, w3, pos, offs, pos1, pos2, own):
    xq = unpack_weight(x_words, x_scales)[:, unstriped(offs)]
    rr = sigmoid(mxq(f64(w3), 0, "e4m3").T @ xq)
    vv = mxq(f64(w2), 0, "e4m3").T @ xq
    kk = mxq(f64(w1), 0, "e4m3").T @ xq
    e0 = np.exp(kk[:, unstriped(pos1)] + f64(pos)[0, :1])
    e1 = np.exp(kk[:, unstriped(pos2)] + f64(pos)[1, :1])
    num = vv[:, unstriped(pos1)] * e0 + vv[:, unstriped(pos2)] * e1
    den = e0 + e1
    out_0 = rr[:, unstriped(own)] * (num / den)
    return (out_0,) + planes(out_0)

@@ -1,0 +1,248 @@
+from contextlib import ExitStack
+
+import concourse.mybir as mybir
+
+K, T, S, V, N = 1024, 2048, 512, 256, 512
+FLOPS = 3 * 2 * K * N * S
+
+F32 = mybir.dt.float32
+BF16 = mybir.dt.bfloat16
+I32 = mybir.dt.int32
+U32 = mybir.dt.uint32
+U16 = mybir.dt.uint16
+U8 = mybir.dt.uint8
+FP8X4 = mybir.dt.float8_e4m3fn_x4
+ALU = mybir.AluOpType
+ACT = mybir.ActivationFunctionType
+
+P = 128
+PACK = 4
+K_PASS = P * PACK
+PASSES = K // K_PASS
+QUADS = 4
+PLACE = {
+    "grouped21": 4160, "mean1": 4160,
+    "raw11": 8192, "share10": 8192, "share01": 9216, "share11": 10240, "shares23": 11328, "share00": 15360,
+    "grouped20": 16320,
+    "grouped10": 20480, "lead1": 20480,
+    "grouped11": 24576, "first3": 24576, "lead23": 25600,
+    "raw21": 28672, "res12": 28672, "res13": 30720,
+}
+ROWS = 4
+
+
+def tile_picked_yaft_aft_po_kernel(
+    tc, x_words, x_scales, w1, w2, w3, pos, offs, pos1, pos2, own, out_0, out_1, out_2
+):
+    nc = tc.nc
+    weights = (w1, w2, w3)
+    with ExitStack() as ctx:
+        keep = ctx.enter_context(tc.tile_pool(name="keep", bufs=1))
+        arena = ctx.enter_context(tc.tile_pool(name="arena", bufs=1))
+        psum = ctx.enter_context(tc.psum_pool(name="psum", bufs=1))
+
+        def fresh(shape, dtype, name):
+            if name in PLACE:
+                return arena.tile(shape, dtype, name=name, offset=PLACE[name], align_bytes=64)
+            return keep.tile(shape, dtype, name=name, align_bytes=64)
+
+        def load_list(name, src):
+            tile = keep.tile(list(src.shape), U16, name=name)
+            nc.sync.dma_start(tile[:], src)
+            return tile
+
+        def load_weight(i, g):
+            raw = fresh([P, PACK, N], F32, "raw%d%d" % (i, g))
+            rows = weights[i][g * K_PASS : (g + 1) * K_PASS, :]
+            nc.sync.dma_start(raw[:], rows.rearrange("(p j) c -> p j c", j=PACK))
+            return raw
+
+        def load_words(g):
+            tile = keep.tile([P, T], I32, name="x_all%d" % g)
+            nc.sync.dma_start(tile[:], x_words[g].rearrange("p n t -> p (n t)").bitcast(I32))
+            return tile
+
+        scale_all = keep.tile([P, T], U8, name="scale_all")
+        nc.vector.memset(scale_all[:].bitcast(I32), 0)
+        raw = {}
+        raw[0, 0] = load_weight(0, 0)
+        offs_sb = load_list("offs_sb", offs)
+        pos1_sb = load_list("pos1_sb", pos1)
+        pos2_sb = load_list("pos2_sb", pos2)
+        own_sb = load_list("own_sb", own)
+        for q in range(QUADS):
+            nc.scalar.dma_start(
+                scale_all[32 * q : 32 * q + PASSES * ROWS, :].bitcast(I32),
+                x_scales[:, ROWS * q : ROWS * (q + 1), :].bitcast(I32),
+            )
+        raw[0, 1] = load_weight(0, 1)
+        x_all = [load_words(g) for g in range(PASSES)]
+        pos_sb = keep.tile([P, 2, V], F32, name="pos_sb")
+        nc.sync.dma_start(pos_sb[:], pos.rearrange("d p v -> p d v"))
+        for i in (1, 2):
+            for g in range(PASSES):
+                raw[i, g] = load_weight(i, g)
+
+        grouped = {}
+        codes = {}
+        scales = {}
+
+        def round_weight(i, g, engine, m0, m1):
+            if (i, g) not in grouped:
+                grouped[i, g] = fresh([P, N * PACK], BF16, "grouped%d%d" % (i, g))
+            dst = grouped[i, g][:].rearrange("p (t m j) -> p m j t", t=PACK, j=PACK)[:, m0:m1]
+            src = raw[i, g][:].rearrange("p j (m t) -> p m j t", t=PACK)[:, m0:m1]
+            if engine is nc.scalar:
+                nc.scalar.copy(dst, src)
+            else:
+                nc.vector.tensor_copy(dst, src)
+
+        def quantize_weight(i, g):
+            codes[i, g] = fresh([P, N], U32, "codes%d%d" % (i, g))
+            scales[i, g] = keep.tile([P, N], U8, name="scales%d%d" % (i, g), align_bytes=64)
+            nc.vector.quantize_mx(out=codes[i, g][:].bitcast(FP8X4), scales=scales[i, g][:], in_=grouped[i, g][:])
+
+        x_scale = keep.tile([P, S], U8, name="x_scale", align_bytes=64)
+        x_code = [keep.tile([P, S], U32, name="x_code%d" % g, align_bytes=64) for g in range(PASSES)]
+
+        def gather_words(g):
+            nc.vector.tensor_copy(x_code[g][:], x_all[g][:].bitcast(U32).indirect(offs_sb[:]))
+
+        banks = {}
+
+        def multiply(i, g):
+            for t in range(PACK):
+                if g == 0:
+                    banks[i, t] = psum.tile([P, S], F32, name="bank%d%d" % (i, t), tag="bank%d%d" % (i % 2, t))
+                cols = slice(t * P, (t + 1) * P)
+                nc.tensor.matmul_mx(
+                    out=banks[i, t][:],
+                    lhsT=codes[i, g][:, cols].bitcast(FP8X4),
+                    lhsT_scale=scales[i, g][:, cols],
+                    rhs=x_code[g][:].bitcast(FP8X4),
+                    rhs_scale=x_scale[ROWS * g :, :],
+                    start=(g == 0),
+                    stop=(g == PASSES - 1),
+                )
+
+        def leave_bank(i, t, func):
+            tile = fresh([P, S], F32, "res%d%d" % (i, t))
+            nc.scalar.activation(tile[:], banks[i, t][:], func)
+            return tile
+
+        round_weight(0, 0, nc.vector, 0, P)
+        nc.vector.tensor_copy(x_scale[:], scale_all[:].indirect(offs_sb[:]))
+        quantize_weight(0, 0)
+        round_weight(0, 1, nc.scalar, 0, P)
+        gather_words(0)
+        multiply(0, 0)
+        quantize_weight(0, 1)
+        gather_words(1)
+        multiply(0, 1)
+        bias = keep.tile([P, V], F32, name="bias")
+        nc.vector.tensor_tensor(bias[:], pos_sb[:, 0, :], pos_sb[:, 1, :], ALU.subtract)
+
+        kk = [leave_bank(0, t, ACT.Copy) for t in range(PACK)]
+        first, lead, share = {}, {}, {}
+        signs = (-1.0, 1.0)
+
+        def key_first(t):
+            first[t] = fresh([P, V], F32, "first%d" % t)
+            nc.vector.tensor_tensor(first[t][:], kk[t][:].indirect(pos1_sb[:]), bias[:], ALU.add)
+
+        def key_second(t):
+            nc.vector.tensor_tensor(lead[t], kk[t][:].indirect(pos2_sb[:]), first[t][:], ALU.subtract)
+
+        def shares(t):
+            for d in range(2):
+                share[d, t] = fresh([P, V], F32, "share%d%d" % (d, t))[:]
+                nc.scalar.activation(share[d, t], lead[t], ACT.Sigmoid, scale=signs[d])
+
+        part, mean, vv, gate = {}, {}, {}, {}
+        lists = (pos1_sb, pos2_sb)
+
+        def value_part(d, t):
+            part[d, t] = fresh([P, V], F32, "part%d%d" % (d, t))
+            nc.vector.tensor_tensor(part[d, t][:], vv[t][:].indirect(lists[d][:]), share[d, t], ALU.mult)
+
+        def value_sum(t):
+            mean[t] = fresh([P, V], F32, "mean%d" % t)
+            nc.vector.tensor_tensor(mean[t][:], part[0, t][:], part[1, t][:], ALU.add)
+
+        key_first(0)
+        round_weight(1, 0, nc.vector, 40, P)
+        round_weight(1, 0, nc.scalar, 0, 40)
+        key_first(1)
+        round_weight(1, 1, nc.scalar, 0, P)
+        lead[0] = fresh([P, V], F32, "lead0")[:]
+        key_second(0)
+        quantize_weight(1, 0)
+        multiply(1, 0)
+        lead[1] = fresh([P, V], F32, "lead1")[:]
+        key_second(1)
+        key_first(2)
+        quantize_weight(1, 1)
+        multiply(1, 1)
+        shares(0)
+        shares(1)
+        key_first(3)
+        lead23 = fresh([P, 2, V], F32, "lead23")
+        lead[2], lead[3] = lead23[:, 0, :], lead23[:, 1, :]
+        key_second(2)
+        vv[0] = leave_bank(1, 0, ACT.Copy)
+        vv[1] = leave_bank(1, 1, ACT.Copy)
+        value_part(0, 0)
+        key_second(3)
+        round_weight(2, 0, nc.scalar, 0, 48)
+        shares23 = fresh([P, 2, 2, V], F32, "shares23")
+        for d in range(2):
+            nc.scalar.activation(shares23[:, d, :, :], lead23[:], ACT.Sigmoid, scale=signs[d])
+            share[d, 2], share[d, 3] = shares23[:, d, 0, :], shares23[:, d, 1, :]
+        value_part(1, 0)
+        round_weight(2, 1, nc.scalar, 0, P)
+        round_weight(2, 0, nc.vector, 48, P)
+        value_part(0, 1)
+        quantize_weight(2, 0)
+        multiply(2, 0)
+        value_part(1, 1)
+        value_sum(0)
+        quantize_weight(2, 1)
+        multiply(2, 1)
+        vv[2] = leave_bank(1, 2, ACT.Copy)
+        vv[3] = leave_bank(1, 3, ACT.Copy)
+        value_sum(1)
+        for t in (2, 3):
+            value_part(0, t)
+            value_part(1, t)
+
+        result = keep.tile([P, PACK, V], F32, name="result")
+        out_rows = out_0.rearrange("(p t) v -> p t v", t=PACK)
+        for t in range(PACK - 1):
+            rr = leave_bank(2, t, ACT.Copy)
+            gate[t] = fresh([P, V], F32, "gate%d" % t)
+            nc.scalar.activation(gate[t][:], rr[:].indirect(own_sb[:]), ACT.Sigmoid)
+        rr = leave_bank(2, PACK - 1, ACT.Sigmoid)
+        nc.vector.tensor_tensor(result[:, 0, :], gate[0][:], mean[0][:], ALU.mult)
+        value_sum(2)
+        nc.vector.tensor_tensor(result[:, 1, :], gate[1][:], mean[1][:], ALU.mult)
+        value_sum(3)
+        nc.vector.tensor_tensor(result[:, 2, :], gate[2][:], mean[2][:], ALU.mult)
+        nc.vector.tensor_tensor(result[:, 3, :], rr[:].indirect(own_sb[:]), mean[3][:], ALU.mult)
+        for t in range(PACK):
+            nc.sync.dma_start(out_rows[:, t, :], result[:, t, :])
+
+        out_grouped = keep.tile([P, V * PACK], BF16, name="out_grouped", align_bytes=64)
+        dst = out_grouped[:].rearrange("p (c i t) -> p c t i", i=4, t=PACK)
+        src = result[:].rearrange("p t (c i) -> p c t i", i=4)
+        nc.vector.tensor_copy(dst[:, 20:], src[:, 20:])
+        nc.scalar.copy(dst[:, :20], src[:, :20])
+        out_codes = keep.tile([P, V], U32, name="out_codes", align_bytes=64)
+        out_scales = keep.tile([P, V], U8, name="out_scales", align_bytes=64)
+        nc.vector.quantize_mx(out=out_codes[:].bitcast(FP8X4), scales=out_scales[:], in_=out_grouped[:])
+        nc.sync.dma_start(out_1[0].rearrange("p n t -> p (n t)").bitcast(I32), out_codes[:].bitcast(I32))
+        for q in range(QUADS):
+            queue = nc.scalar if q % 2 == 0 else nc.sync
+            queue.dma_start(
+                out_2[0, ROWS * q : ROWS * (q + 1), :].bitcast(I32),
+                out_scales[32 * q : 32 * q + ROWS, :].bitcast(I32),
+            )

@@ -27,6 +27,8 @@ PLACE = {
     "grouped10": 20480, "lead1": 20480,
     "grouped11": 24576, "first3": 24576, "lead23": 25600,
     "raw21": 28672, "res12": 28672, "res13": 30720,
+    "warm": 4096, "scale_all": 0, "codes01": 0,
+    "raw10": 36864, "raw20": 45056, "x_all0": 53248, "x_all1": 61440, "pos_sb": 69632, "bias": 61440,
 }
 ROWS = 4
 
@@ -58,26 +60,30 @@ def tile_picked_yaft_aft_po_kernel(
             return raw
 
         def load_words(g):
-            tile = keep.tile([P, T], I32, name="x_all%d" % g)
+            tile = fresh([P, T], I32, "x_all%d" % g)
             nc.sync.dma_start(tile[:], x_words[g].rearrange("p n t -> p (n t)").bitcast(I32))
             return tile
 
-        scale_all = keep.tile([P, T], U8, name="scale_all")
-        nc.vector.memset(scale_all[:].bitcast(I32), 0)
+        scale_all = fresh([P, T // 4], I32, "scale_all")
+        nc.vector.memset(scale_all[:], 0)
+        warm = fresh([P, (71680 - 4096) // 4], F32, "warm")
+        nc.vector.memset(warm[:, 0:1], 0.0)
+        warm_out = fresh([P, 1], F32, "warm_out")
+        nc.scalar.activation(warm_out[:], warm[:, 0:1], ACT.Sigmoid)
         raw = {}
         raw[0, 0] = load_weight(0, 0)
         offs_sb = load_list("offs_sb", offs)
         pos1_sb = load_list("pos1_sb", pos1)
         pos2_sb = load_list("pos2_sb", pos2)
         own_sb = load_list("own_sb", own)
+        raw[0, 1] = load_weight(0, 1)
         for q in range(QUADS):
-            nc.scalar.dma_start(
-                scale_all[32 * q : 32 * q + PASSES * ROWS, :].bitcast(I32),
+            nc.sync.dma_start(
+                scale_all[32 * q : 32 * q + PASSES * ROWS, :],
                 x_scales[:, ROWS * q : ROWS * (q + 1), :].bitcast(I32),
             )
-        raw[0, 1] = load_weight(0, 1)
         x_all = [load_words(g) for g in range(PASSES)]
-        pos_sb = keep.tile([P, 2, V], F32, name="pos_sb")
+        pos_sb = fresh([P, 2, V], F32, "pos_sb")
         nc.sync.dma_start(pos_sb[:], pos.rearrange("d p v -> p d v"))
         for i in (1, 2):
             for g in range(PASSES):
@@ -131,7 +137,7 @@ def tile_picked_yaft_aft_po_kernel(
             return tile
 
         round_weight(0, 0, nc.vector, 0, P)
-        nc.vector.tensor_copy(x_scale[:], scale_all[:].indirect(offs_sb[:]))
+        nc.vector.tensor_copy(x_scale[:], scale_all[:].bitcast(U8).indirect(offs_sb[:]))
         quantize_weight(0, 0)
         round_weight(0, 1, nc.scalar, 0, P)
         gather_words(0)
@@ -139,7 +145,7 @@ def tile_picked_yaft_aft_po_kernel(
         quantize_weight(0, 1)
         gather_words(1)
         multiply(0, 1)
-        bias = keep.tile([P, V], F32, name="bias")
+        bias = fresh([P, V], F32, "bias")
         nc.vector.tensor_tensor(bias[:], pos_sb[:, 0, :], pos_sb[:, 1, :], ALU.subtract)
 
         kk = [leave_bank(0, t, ACT.Copy) for t in range(PACK)]
@@ -193,14 +199,14 @@ def tile_picked_yaft_aft_po_kernel(
         vv[1] = leave_bank(1, 1, ACT.Copy)
         value_part(0, 0)
         key_second(3)
-        round_weight(2, 0, nc.scalar, 0, 48)
+        round_weight(2, 0, nc.scalar, 0, 24)
         shares23 = fresh([P, 2, 2, V], F32, "shares23")
         for d in range(2):
             nc.scalar.activation(shares23[:, d, :, :], lead23[:], ACT.Sigmoid, scale=signs[d])
             share[d, 2], share[d, 3] = shares23[:, d, 0, :], shares23[:, d, 1, :]
         value_part(1, 0)
         round_weight(2, 1, nc.scalar, 0, P)
-        round_weight(2, 0, nc.vector, 48, P)
+        round_weight(2, 0, nc.vector, 24, P)
         value_part(0, 1)
         quantize_weight(2, 0)
         multiply(2, 0)

@@ -25,7 +25,7 @@ PLACE = {
     "raw11": 8192, "share10": 8192, "share01": 9216, "share11": 10240, "shares23": 11328, "share00": 15360,
     "grouped20": 16320,
     "grouped10": 20480, "lead1": 20480,
-    "grouped11": 24576, "first3": 24576, "lead23": 25600,
+    "grouped11": 24576, "lead23": 25600,
     "raw21": 28672, "res12": 28672, "res13": 30720,
     "warm": 4096, "scale_all": 0, "codes01": 0,
     "raw10": 36864, "raw20": 45056, "x_all0": 53248, "x_all1": 61440, "pos_sb": 69632, "bias": 61440,
@@ -96,8 +96,8 @@ def tile_picked_yaft_aft_po_kernel(
         def round_weight(i, g, engine, m0, m1):
             if (i, g) not in grouped:
                 grouped[i, g] = fresh([P, N * PACK], BF16, "grouped%d%d" % (i, g))
-            dst = grouped[i, g][:].rearrange("p (t m j) -> p m j t", t=PACK, j=PACK)[:, m0:m1]
-            src = raw[i, g][:].rearrange("p j (m t) -> p m j t", t=PACK)[:, m0:m1]
+            dst = grouped[i, g][:].rearrange("p (h u m j) -> p h m j u", h=2, u=2, j=PACK)[:, :, m0:m1]
+            src = raw[i, g][:].rearrange("p j (m h u) -> p h m j u", h=2, u=2)[:, :, m0:m1]
             if engine is nc.scalar:
                 nc.scalar.copy(dst, src)
             else:
@@ -133,13 +133,17 @@ def tile_picked_yaft_aft_po_kernel(
 
         def leave_bank(i, t, func):
             tile = fresh([P, S], F32, "res%d%d" % (i, t))
-            nc.scalar.activation(tile[:], banks[i, t][:], func)
+            if func is None:
+                nc.scalar.copy(tile[:], banks[i, t][:])
+            else:
+                nc.scalar.activation(tile[:], banks[i, t][:], func)
             return tile
 
         round_weight(0, 0, nc.vector, 0, P)
         nc.vector.tensor_copy(x_scale[:], scale_all[:].bitcast(U8).indirect(offs_sb[:]))
         quantize_weight(0, 0)
-        round_weight(0, 1, nc.scalar, 0, P)
+        round_weight(0, 1, nc.scalar, 0, 64)
+        round_weight(0, 1, nc.vector, 64, P)
         gather_words(0)
         multiply(0, 0)
         quantize_weight(0, 1)
@@ -148,7 +152,7 @@ def tile_picked_yaft_aft_po_kernel(
         bias = fresh([P, V], F32, "bias")
         nc.vector.tensor_tensor(bias[:], pos_sb[:, 0, :], pos_sb[:, 1, :], ALU.subtract)
 
-        kk = [leave_bank(0, t, ACT.Copy) for t in range(PACK)]
+        kk = [leave_bank(0, t, None) for t in range(PACK)]
         first, lead, share = {}, {}, {}
         signs = (-1.0, 1.0)
 
@@ -195,8 +199,8 @@ def tile_picked_yaft_aft_po_kernel(
         lead23 = fresh([P, 2, V], F32, "lead23")
         lead[2], lead[3] = lead23[:, 0, :], lead23[:, 1, :]
         key_second(2)
-        vv[0] = leave_bank(1, 0, ACT.Copy)
-        vv[1] = leave_bank(1, 1, ACT.Copy)
+        vv[0] = leave_bank(1, 0, None)
+        vv[1] = leave_bank(1, 1, None)
         value_part(0, 0)
         key_second(3)
         round_weight(2, 0, nc.scalar, 0, 24)
@@ -214,8 +218,8 @@ def tile_picked_yaft_aft_po_kernel(
         value_sum(0)
         quantize_weight(2, 1)
         multiply(2, 1)
-        vv[2] = leave_bank(1, 2, ACT.Copy)
-        vv[3] = leave_bank(1, 3, ACT.Copy)
+        vv[2] = leave_bank(1, 2, None)
+        vv[3] = leave_bank(1, 3, None)
         value_sum(1)
         for t in (2, 3):
             value_part(0, t)
@@ -224,7 +228,7 @@ def tile_picked_yaft_aft_po_kernel(
         result = keep.tile([P, PACK, V], F32, name="result")
         out_rows = out_0.rearrange("(p t) v -> p t v", t=PACK)
         for t in range(PACK - 1):
-            rr = leave_bank(2, t, ACT.Copy)
+            rr = leave_bank(2, t, None)
             gate[t] = fresh([P, V], F32, "gate%d" % t)
             nc.scalar.activation(gate[t][:], rr[:].indirect(own_sb[:]), ACT.Sigmoid)
         rr = leave_bank(2, PACK - 1, ACT.Sigmoid)

@@ -20,17 +20,18 @@ PACK = 4
 K_PASS = P * PACK
 PASSES = K // K_PASS
 QUADS = 4
-PLACE = {
-    "grouped21": 4160, "mean1": 4160,
-    "raw11": 8192, "share10": 8192, "share01": 9216, "share11": 10240, "shares23": 11328, "share00": 15360,
-    "grouped20": 16320,
-    "grouped10": 20480, "lead1": 20480,
-    "grouped11": 24576, "lead23": 25600,
-    "raw21": 28672, "res12": 28672, "res13": 30720,
-    "warm": 4096, "scale_all": 0, "codes01": 0,
-    "raw10": 36864, "raw20": 45056, "x_all0": 53248, "x_all1": 61440, "pos_sb": 69632, "bias": 61440,
-}
 ROWS = 4
+RAW = PACK * N * 4
+PLACE = {
+    "warm": 0,
+    "raw10": 0, "lead01": 0,
+    "raw11": RAW, "first3": RAW, "lead23": RAW + 1024,
+    "raw20": 2 * RAW, "shares01": 2 * RAW,
+    "raw21": 3 * RAW, "part11": 3 * RAW,
+    "x_all0": 4 * RAW, "x_all1": 5 * RAW, "bias": 5 * RAW,
+    "pos_sb": 6 * RAW,
+    "scale_all": 6 * RAW + 2048, "codes01": 6 * RAW + 2048,
+}
 
 
 def tile_picked_yaft_aft_po_kernel(
@@ -66,7 +67,7 @@ def tile_picked_yaft_aft_po_kernel(
 
         scale_all = fresh([P, T // 4], I32, "scale_all")
         nc.vector.memset(scale_all[:], 0)
-        warm = fresh([P, (71680 - 4096) // 4], F32, "warm")
+        warm = fresh([P, (6 * RAW + 2048) // 4], F32, "warm")
         nc.vector.memset(warm[:, 0:1], 0.0)
         warm_out = fresh([P, 1], F32, "warm_out")
         nc.scalar.activation(warm_out[:], warm[:, 0:1], ACT.Sigmoid)
@@ -92,11 +93,14 @@ def tile_picked_yaft_aft_po_kernel(
         grouped = {}
         codes = {}
         scales = {}
+        grouped_w2 = fresh([P, PASSES * N * PACK], BF16, "grouped_w2")
+        for g in range(PASSES):
+            grouped[1, g] = grouped_w2[:, g * N * PACK : (g + 1) * N * PACK]
 
         def round_weight(i, g, engine, m0, m1):
             if (i, g) not in grouped:
-                grouped[i, g] = fresh([P, N * PACK], BF16, "grouped%d%d" % (i, g))
-            dst = grouped[i, g][:].rearrange("p (h u m j) -> p h m j u", h=2, u=2, j=PACK)[:, :, m0:m1]
+                grouped[i, g] = fresh([P, N * PACK], BF16, "grouped%d%d" % (i, g))[:]
+            dst = grouped[i, g].rearrange("p (h u m j) -> p h m j u", h=2, u=2, j=PACK)[:, :, m0:m1]
             src = raw[i, g][:].rearrange("p j (m h u) -> p h m j u", h=2, u=2)[:, :, m0:m1]
             if engine is nc.scalar:
                 nc.scalar.copy(dst, src)
@@ -104,9 +108,17 @@ def tile_picked_yaft_aft_po_kernel(
                 nc.vector.tensor_copy(dst, src)
 
         def quantize_weight(i, g):
-            codes[i, g] = fresh([P, N], U32, "codes%d%d" % (i, g))
-            scales[i, g] = keep.tile([P, N], U8, name="scales%d%d" % (i, g), align_bytes=64)
-            nc.vector.quantize_mx(out=codes[i, g][:].bitcast(FP8X4), scales=scales[i, g][:], in_=grouped[i, g][:])
+            codes[i, g] = fresh([P, N], U32, "codes%d%d" % (i, g))[:]
+            scales[i, g] = fresh([P, N], U8, "scales%d%d" % (i, g))[:]
+            nc.vector.quantize_mx(out=codes[i, g].bitcast(FP8X4), scales=scales[i, g], in_=grouped[i, g])
+
+        def quantize_w2():
+            both_codes = fresh([P, PASSES * N], U32, "codes_w2")
+            both_scales = fresh([P, PASSES * N], U8, "scales_w2")
+            nc.vector.quantize_mx(out=both_codes[:].bitcast(FP8X4), scales=both_scales[:], in_=grouped_w2[:])
+            for g in range(PASSES):
+                codes[1, g] = both_codes[:, g * N : (g + 1) * N]
+                scales[1, g] = both_scales[:, g * N : (g + 1) * N]
 
         x_scale = keep.tile([P, S], U8, name="x_scale", align_bytes=64)
         x_code = [keep.tile([P, S], U32, name="x_code%d" % g, align_bytes=64) for g in range(PASSES)]
@@ -116,20 +128,23 @@ def tile_picked_yaft_aft_po_kernel(
 
         banks = {}
 
+        def one_pass(i, g, t):
+            if g == 0:
+                banks[i, t] = psum.tile([P, S], F32, name="bank%d%d" % (i, t), tag="bank%d%d" % (i % 2, t))
+            cols = slice(t * P, (t + 1) * P)
+            nc.tensor.matmul_mx(
+                out=banks[i, t][:],
+                lhsT=codes[i, g][:, cols].bitcast(FP8X4),
+                lhsT_scale=scales[i, g][:, cols],
+                rhs=x_code[g][:].bitcast(FP8X4),
+                rhs_scale=x_scale[ROWS * g :, :],
+                start=(g == 0),
+                stop=(g == PASSES - 1),
+            )
+
         def multiply(i, g):
             for t in range(PACK):
-                if g == 0:
-                    banks[i, t] = psum.tile([P, S], F32, name="bank%d%d" % (i, t), tag="bank%d%d" % (i % 2, t))
-                cols = slice(t * P, (t + 1) * P)
-                nc.tensor.matmul_mx(
-                    out=banks[i, t][:],
-                    lhsT=codes[i, g][:, cols].bitcast(FP8X4),
-                    lhsT_scale=scales[i, g][:, cols],
-                    rhs=x_code[g][:].bitcast(FP8X4),
-                    rhs_scale=x_scale[ROWS * g :, :],
-                    start=(g == 0),
-                    stop=(g == PASSES - 1),
-                )
+                one_pass(i, g, t)
 
         def leave_bank(i, t, func):
             tile = fresh([P, S], F32, "res%d%d" % (i, t))
@@ -139,14 +154,15 @@ def tile_picked_yaft_aft_po_kernel(
                 nc.scalar.activation(tile[:], banks[i, t][:], func)
             return tile
 
-        round_weight(0, 0, nc.vector, 0, P)
-        nc.vector.tensor_copy(x_scale[:], scale_all[:].bitcast(U8).indirect(offs_sb[:]))
+        round_weight(0, 0, nc.scalar, 0, 48)
+        round_weight(0, 0, nc.vector, 48, P)
         quantize_weight(0, 0)
         round_weight(0, 1, nc.scalar, 0, 64)
         round_weight(0, 1, nc.vector, 64, P)
+        nc.vector.tensor_copy(x_scale[:], scale_all[:].bitcast(U8).indirect(offs_sb[:]))
+        quantize_weight(0, 1)
         gather_words(0)
         multiply(0, 0)
-        quantize_weight(0, 1)
         gather_words(1)
         multiply(0, 1)
         bias = fresh([P, V], F32, "bias")
@@ -155,20 +171,24 @@ def tile_picked_yaft_aft_po_kernel(
         kk = [leave_bank(0, t, None) for t in range(PACK)]
         first, lead, share = {}, {}, {}
         signs = (-1.0, 1.0)
+        lead_pair = {0: fresh([P, 2, V], F32, "lead01"), 2: fresh([P, 2, V], F32, "lead23")}
 
         def key_first(t):
             first[t] = fresh([P, V], F32, "first%d" % t)
             nc.vector.tensor_tensor(first[t][:], kk[t][:].indirect(pos1_sb[:]), bias[:], ALU.add)
 
         def key_second(t):
-            nc.vector.tensor_tensor(lead[t], kk[t][:].indirect(pos2_sb[:]), first[t][:], ALU.subtract)
+            nc.vector.tensor_tensor(
+                lead_pair[t - t % 2][:, t % 2, :], kk[t][:].indirect(pos2_sb[:]), first[t][:], ALU.subtract
+            )
 
-        def shares(t):
+        def shares(t0):
+            both = fresh([P, 2, 2, V], F32, "shares%d%d" % (t0, t0 + 1))
             for d in range(2):
-                share[d, t] = fresh([P, V], F32, "share%d%d" % (d, t))[:]
-                nc.scalar.activation(share[d, t], lead[t], ACT.Sigmoid, scale=signs[d])
+                nc.scalar.activation(both[:, d, :, :], lead_pair[t0][:], ACT.Sigmoid, scale=signs[d])
+                share[d, t0], share[d, t0 + 1] = both[:, d, 0, :], both[:, d, 1, :]
 
-        part, mean, vv, gate = {}, {}, {}, {}
+        part, mean, vv, gate, rr = {}, {}, {}, {}, {}
         lists = (pos1_sb, pos2_sb)
 
         def value_part(d, t):
@@ -180,66 +200,70 @@ def tile_picked_yaft_aft_po_kernel(
             nc.vector.tensor_tensor(mean[t][:], part[0, t][:], part[1, t][:], ALU.add)
 
         key_first(0)
-        round_weight(1, 0, nc.vector, 40, P)
-        round_weight(1, 0, nc.scalar, 0, 40)
         key_first(1)
+        round_weight(1, 0, nc.vector, 28, P)
+        round_weight(1, 0, nc.scalar, 0, 28)
         round_weight(1, 1, nc.scalar, 0, P)
-        lead[0] = fresh([P, V], F32, "lead0")[:]
-        key_second(0)
-        quantize_weight(1, 0)
-        multiply(1, 0)
-        lead[1] = fresh([P, V], F32, "lead1")[:]
-        key_second(1)
         key_first(2)
-        quantize_weight(1, 1)
-        multiply(1, 1)
-        shares(0)
-        shares(1)
+        key_second(0)
+        key_second(1)
+        quantize_w2()
+        for t in range(PACK):
+            for g in range(PASSES):
+                one_pass(1, g, t)
+        round_weight(2, 0, nc.scalar, 0, P)
         key_first(3)
-        lead23 = fresh([P, 2, V], F32, "lead23")
-        lead[2], lead[3] = lead23[:, 0, :], lead23[:, 1, :]
         key_second(2)
-        vv[0] = leave_bank(1, 0, None)
-        vv[1] = leave_bank(1, 1, None)
-        value_part(0, 0)
         key_second(3)
-        round_weight(2, 0, nc.scalar, 0, 24)
-        shares23 = fresh([P, 2, 2, V], F32, "shares23")
-        for d in range(2):
-            nc.scalar.activation(shares23[:, d, :, :], lead23[:], ACT.Sigmoid, scale=signs[d])
-            share[d, 2], share[d, 3] = shares23[:, d, 0, :], shares23[:, d, 1, :]
-        value_part(1, 0)
-        round_weight(2, 1, nc.scalar, 0, P)
-        round_weight(2, 0, nc.vector, 24, P)
-        value_part(0, 1)
+        vv[0] = leave_bank(1, 0, None)
+        shares(0)
+        vv[1] = leave_bank(1, 1, None)
         quantize_weight(2, 0)
         multiply(2, 0)
-        value_part(1, 1)
+        round_weight(2, 1, nc.vector, 96, P)
+        round_weight(2, 1, nc.scalar, 0, 96)
+        value_part(0, 0)
+        value_part(1, 0)
+        value_part(0, 1)
         value_sum(0)
         quantize_weight(2, 1)
         multiply(2, 1)
+        shares(2)
         vv[2] = leave_bank(1, 2, None)
         vv[3] = leave_bank(1, 3, None)
+        value_part(1, 1)
+        value_part(0, 2)
         value_sum(1)
-        for t in (2, 3):
-            value_part(0, t)
-            value_part(1, t)
+        value_part(1, 2)
+        value_part(0, 3)
+        value_sum(2)
+        value_part(1, 3)
 
         result = keep.tile([P, PACK, V], F32, name="result")
         out_rows = out_0.rearrange("(p t) v -> p t v", t=PACK)
-        for t in range(PACK - 1):
-            rr = leave_bank(2, t, None)
+
+        def gate_on_scalar(t):
             gate[t] = fresh([P, V], F32, "gate%d" % t)
-            nc.scalar.activation(gate[t][:], rr[:].indirect(own_sb[:]), ACT.Sigmoid)
-        rr = leave_bank(2, PACK - 1, ACT.Sigmoid)
-        nc.vector.tensor_tensor(result[:, 0, :], gate[0][:], mean[0][:], ALU.mult)
-        value_sum(2)
-        nc.vector.tensor_tensor(result[:, 1, :], gate[1][:], mean[1][:], ALU.mult)
-        value_sum(3)
-        nc.vector.tensor_tensor(result[:, 2, :], gate[2][:], mean[2][:], ALU.mult)
-        nc.vector.tensor_tensor(result[:, 3, :], rr[:].indirect(own_sb[:]), mean[3][:], ALU.mult)
-        for t in range(PACK):
+            nc.scalar.activation(gate[t][:], rr[t][:].indirect(own_sb[:]), ACT.Sigmoid)
+
+        def finish(t):
+            if t in gate:
+                nc.vector.tensor_tensor(result[:, t, :], gate[t][:], mean[t][:], ALU.mult)
+            else:
+                nc.vector.tensor_tensor(result[:, t, :], rr[t][:].indirect(own_sb[:]), mean[t][:], ALU.mult)
             nc.sync.dma_start(out_rows[:, t, :], result[:, t, :])
+
+        rr[0] = leave_bank(2, 0, None)
+        rr[1] = leave_bank(2, 1, None)
+        gate_on_scalar(0)
+        rr[2] = leave_bank(2, 2, ACT.Sigmoid)
+        gate_on_scalar(1)
+        rr[3] = leave_bank(2, 3, ACT.Sigmoid)
+        finish(0)
+        value_sum(3)
+        finish(2)
+        finish(1)
+        finish(3)
 
         out_grouped = keep.tile([P, V * PACK], BF16, name="out_grouped", align_bytes=64)
         dst = out_grouped[:].rearrange("p (c i t) -> p c t i", i=4, t=PACK)

@@ -23,14 +23,10 @@ QUADS = 4
 ROWS = 4
 RAW = PACK * N * 4
 PLACE = {
-    "warm": 0,
-    "raw10": 0, "lead01": 0,
-    "raw11": RAW, "first3": RAW, "lead23": RAW + 1024,
-    "raw20": 2 * RAW, "shares01": 2 * RAW,
-    "raw21": 3 * RAW, "part11": 3 * RAW,
-    "x_all0": 4 * RAW, "x_all1": 5 * RAW, "bias": 5 * RAW,
-    "pos_sb": 6 * RAW,
-    "scale_all": 6 * RAW + 2048, "codes01": 6 * RAW + 2048,
+    "raw11": 0, "shares01": 0,
+    "lead01": RAW, "lead23": RAW,
+    "raw21": 2 * RAW, "part11": 2 * RAW,
+    "x_all1": 3 * RAW, "bias": 3 * RAW,
 }
 
 
@@ -54,11 +50,14 @@ def tile_picked_yaft_aft_po_kernel(
             nc.sync.dma_start(tile[:], src)
             return tile
 
-        def load_weight(i, g):
-            raw = fresh([P, PACK, N], F32, "raw%d%d" % (i, g))
-            rows = weights[i][g * K_PASS : (g + 1) * K_PASS, :]
-            nc.sync.dma_start(raw[:], rows.rearrange("(p j) c -> p j c", j=PACK))
-            return raw
+        raw = {}
+
+        def load_weight(i, g, m0=0, m1=P):
+            name = "raw%d%d" % (i, g) if m1 - m0 == P else "raw%d%d_%d" % (i, g, m0)
+            tile = fresh([P, PACK, PACK * (m1 - m0)], F32, name)
+            rows = weights[i][g * K_PASS : (g + 1) * K_PASS, PACK * m0 : PACK * m1]
+            nc.sync.dma_start(tile[:], rows.rearrange("(p j) c -> p j c", j=PACK))
+            raw.setdefault((i, g), []).append((m0, m1, tile))
 
         def load_words(g):
             tile = fresh([P, T], I32, "x_all%d" % g)
@@ -67,28 +66,30 @@ def tile_picked_yaft_aft_po_kernel(
 
         scale_all = fresh([P, T // 4], I32, "scale_all")
         nc.vector.memset(scale_all[:], 0)
-        warm = fresh([P, (6 * RAW + 2048) // 4], F32, "warm")
-        nc.vector.memset(warm[:, 0:1], 0.0)
+        warm = fresh([P, 1], F32, "warm_in")
+        nc.vector.memset(warm[:], 0.0)
         warm_out = fresh([P, 1], F32, "warm_out")
-        nc.scalar.activation(warm_out[:], warm[:, 0:1], ACT.Sigmoid)
-        raw = {}
-        raw[0, 0] = load_weight(0, 0)
+        nc.scalar.activation(warm_out[:], warm[:], ACT.Sigmoid)
+        load_weight(0, 0)
         offs_sb = load_list("offs_sb", offs)
-        pos1_sb = load_list("pos1_sb", pos1)
-        pos2_sb = load_list("pos2_sb", pos2)
-        own_sb = load_list("own_sb", own)
-        raw[0, 1] = load_weight(0, 1)
+        x_all = [load_words(0)]
         for q in range(QUADS):
             nc.sync.dma_start(
                 scale_all[32 * q : 32 * q + PASSES * ROWS, :],
                 x_scales[:, ROWS * q : ROWS * (q + 1), :].bitcast(I32),
             )
-        x_all = [load_words(g) for g in range(PASSES)]
+        load_weight(0, 1)
+        x_all.append(load_words(1))
+        pos1_sb = load_list("pos1_sb", pos1)
+        load_weight(1, 0, 0, 64)
         pos_sb = fresh([P, 2, V], F32, "pos_sb")
         nc.sync.dma_start(pos_sb[:], pos.rearrange("d p v -> p d v"))
-        for i in (1, 2):
-            for g in range(PASSES):
-                raw[i, g] = load_weight(i, g)
+        load_weight(1, 0, 64, P)
+        pos2_sb = load_list("pos2_sb", pos2)
+        load_weight(1, 1)
+        for g in range(PASSES):
+            load_weight(2, g)
+        own_sb = load_list("own_sb", own)
 
         grouped = {}
         codes = {}
@@ -101,7 +102,8 @@ def tile_picked_yaft_aft_po_kernel(
             if (i, g) not in grouped:
                 grouped[i, g] = fresh([P, N * PACK], BF16, "grouped%d%d" % (i, g))[:]
             dst = grouped[i, g].rearrange("p (h u m j) -> p h m j u", h=2, u=2, j=PACK)[:, :, m0:m1]
-            src = raw[i, g][:].rearrange("p j (m h u) -> p h m j u", h=2, u=2)[:, :, m0:m1]
+            start, tile = [(a, tile) for a, b, tile in raw[i, g] if a <= m0 and m1 <= b][0]
+            src = tile[:].rearrange("p j (m h u) -> p h m j u", h=2, u=2)[:, :, m0 - start : m1 - start]
             if engine is nc.scalar:
                 nc.scalar.copy(dst, src)
             else:
@@ -123,8 +125,10 @@ def tile_picked_yaft_aft_po_kernel(
         x_scale = keep.tile([P, S], U8, name="x_scale", align_bytes=64)
         x_code = [keep.tile([P, S], U32, name="x_code%d" % g, align_bytes=64) for g in range(PASSES)]
 
-        def gather_words(g):
-            nc.vector.tensor_copy(x_code[g][:], x_all[g][:].bitcast(U32).indirect(offs_sb[:]))
+        def gather_words(g, j0=0, j1=S):
+            nc.vector.tensor_copy(
+                x_code[g][:, j0:j1], x_all[g][:].bitcast(U32).indirect(offs_sb[:, j0 // 16 : j1 // 16])
+            )
 
         banks = {}
 
@@ -138,6 +142,22 @@ def tile_picked_yaft_aft_po_kernel(
                 lhsT_scale=scales[i, g][:, cols],
                 rhs=x_code[g][:].bitcast(FP8X4),
                 rhs_scale=x_scale[ROWS * g :, :],
+                start=(g == 0),
+                stop=(g == PASSES - 1),
+            )
+
+        halves = (slice(0, S // 2), slice(S // 2, S))
+        half_banks = [
+            psum.tile([P, S // 2], F32, name="half_bank%d" % h, tag=("bank00", "bank13")[h]) for h in range(2)
+        ]
+
+        def half_pass(g, h):
+            nc.tensor.matmul_mx(
+                out=half_banks[h][:],
+                lhsT=codes[0, g][:, 0:P].bitcast(FP8X4),
+                lhsT_scale=scales[0, g][:, 0:P],
+                rhs=x_code[g][:, halves[h]].bitcast(FP8X4),
+                rhs_scale=x_scale[ROWS * g :, halves[h]],
                 start=(g == 0),
                 stop=(g == PASSES - 1),
             )
@@ -157,18 +177,28 @@ def tile_picked_yaft_aft_po_kernel(
         round_weight(0, 0, nc.scalar, 0, 48)
         round_weight(0, 0, nc.vector, 48, P)
         quantize_weight(0, 0)
+        gather_words(0)
+        nc.vector.tensor_copy(x_scale[:], scale_all[:].bitcast(U8).indirect(offs_sb[:]))
+        half_pass(0, 0)
+        half_pass(0, 1)
+        for t in range(1, PACK):
+            one_pass(0, 0, t)
         round_weight(0, 1, nc.scalar, 0, 64)
         round_weight(0, 1, nc.vector, 64, P)
-        nc.vector.tensor_copy(x_scale[:], scale_all[:].bitcast(U8).indirect(offs_sb[:]))
         quantize_weight(0, 1)
-        gather_words(0)
-        multiply(0, 0)
-        gather_words(1)
-        multiply(0, 1)
+        for h in range(2):
+            gather_words(1, halves[h].start, halves[h].stop)
+            half_pass(1, h)
+        for t in range(1, PACK):
+            one_pass(0, 1, t)
+        round_weight(1, 0, nc.vector, 0, 64)
         bias = fresh([P, V], F32, "bias")
         nc.vector.tensor_tensor(bias[:], pos_sb[:, 0, :], pos_sb[:, 1, :], ALU.subtract)
 
-        kk = [leave_bank(0, t, None) for t in range(PACK)]
+        kk = [fresh([P, S], F32, "res00")]
+        for h in range(2):
+            nc.scalar.copy(kk[0][:, halves[h]], half_banks[h][:])
+        kk.extend(leave_bank(0, t, None) for t in range(1, PACK))
         first, lead, share = {}, {}, {}
         signs = (-1.0, 1.0)
         lead_pair = {0: fresh([P, 2, V], F32, "lead01"), 2: fresh([P, 2, V], F32, "lead23")}
@@ -200,28 +230,29 @@ def tile_picked_yaft_aft_po_kernel(
             nc.vector.tensor_tensor(mean[t][:], part[0, t][:], part[1, t][:], ALU.add)
 
         key_first(0)
+        round_weight(1, 0, nc.scalar, 64, P)
+        round_weight(1, 1, nc.scalar, 0, 96)
         key_first(1)
-        round_weight(1, 0, nc.vector, 28, P)
-        round_weight(1, 0, nc.scalar, 0, 28)
-        round_weight(1, 1, nc.scalar, 0, P)
-        key_first(2)
         key_second(0)
+        key_first(2)
         key_second(1)
+        key_first(3)
+        round_weight(1, 1, nc.vector, 96, P)
         quantize_w2()
         for t in range(PACK):
             for g in range(PASSES):
                 one_pass(1, g, t)
-        round_weight(2, 0, nc.scalar, 0, P)
-        key_first(3)
+        shares(0)
+        round_weight(2, 0, nc.scalar, 0, 84)
         key_second(2)
         key_second(3)
+        round_weight(2, 0, nc.vector, 84, P)
         vv[0] = leave_bank(1, 0, None)
-        shares(0)
         vv[1] = leave_bank(1, 1, None)
+        round_weight(2, 1, nc.vector, 104, P)
         quantize_weight(2, 0)
         multiply(2, 0)
-        round_weight(2, 1, nc.vector, 96, P)
-        round_weight(2, 1, nc.scalar, 0, 96)
+        round_weight(2, 1, nc.scalar, 0, 104)
         value_part(0, 0)
         value_part(1, 0)
         value_part(0, 1)

@@ -183,8 +183,8 @@ def tile_picked_yaft_aft_po_kernel(
         half_pass(0, 1)
         for t in range(1, PACK):
             one_pass(0, 0, t)
-        round_weight(0, 1, nc.scalar, 0, 64)
-        round_weight(0, 1, nc.vector, 64, P)
+        round_weight(0, 1, nc.scalar, 0, 40)
+        round_weight(0, 1, nc.vector, 40, P)
         quantize_weight(0, 1)
         for h in range(2):
             gather_words(1, halves[h].start, halves[h].stop)
@@ -249,10 +249,10 @@ def tile_picked_yaft_aft_po_kernel(
         round_weight(2, 0, nc.vector, 84, P)
         vv[0] = leave_bank(1, 0, None)
         vv[1] = leave_bank(1, 1, None)
-        round_weight(2, 1, nc.vector, 104, P)
+        round_weight(2, 1, nc.vector, 72, P)
         quantize_weight(2, 0)
         multiply(2, 0)
-        round_weight(2, 1, nc.scalar, 0, 104)
+        round_weight(2, 1, nc.scalar, 0, 72)
         value_part(0, 0)
         value_part(1, 0)
         value_part(0, 1)
@@ -282,19 +282,19 @@ def tile_picked_yaft_aft_po_kernel(
                 nc.vector.tensor_tensor(result[:, t, :], gate[t][:], mean[t][:], ALU.mult)
             else:
                 nc.vector.tensor_tensor(result[:, t, :], rr[t][:].indirect(own_sb[:]), mean[t][:], ALU.mult)
-            nc.sync.dma_start(out_rows[:, t, :], result[:, t, :])
 
         rr[0] = leave_bank(2, 0, None)
-        rr[1] = leave_bank(2, 1, None)
-        gate_on_scalar(0)
-        rr[2] = leave_bank(2, 2, ACT.Sigmoid)
-        gate_on_scalar(1)
-        rr[3] = leave_bank(2, 3, ACT.Sigmoid)
-        finish(0)
+        for t in range(PACK):
+            if t + 1 < PACK:
+                rr[t + 1] = leave_bank(2, t + 1, None)
+            gate_on_scalar(t)
         value_sum(3)
-        finish(2)
+        finish(0)
         finish(1)
+        nc.sync.dma_start(out_rows[:, 0:2, :], result[:, 0:2, :])
+        finish(2)
         finish(3)
+        nc.sync.dma_start(out_rows[:, 2:4, :], result[:, 2:4, :])
 
         out_grouped = keep.tile([P, V * PACK], BF16, name="out_grouped", align_bytes=64)
         dst = out_grouped[:].rearrange("p (c i t) -> p c t i", i=4, t=PACK)

@@ -24,9 +24,10 @@ ROWS = 4
 RAW = PACK * N * 4
 PLACE = {
     "raw11": 0, "shares01": 0,
-    "lead01": RAW, "lead23": RAW,
+    "lead01": RAW, "lead23": RAW, "mean1": RAW,
     "raw21": 2 * RAW, "part11": 2 * RAW,
     "x_all1": 3 * RAW, "bias": 3 * RAW,
+    "res20": 4 * RAW, "mean3": 4 * RAW,
 }
 
 
@@ -259,8 +260,8 @@ def tile_picked_yaft_aft_po_kernel(
         value_sum(0)
         quantize_weight(2, 1)
         multiply(2, 1)
-        shares(2)
         vv[2] = leave_bank(1, 2, None)
+        shares(2)
         vv[3] = leave_bank(1, 3, None)
         value_part(1, 1)
         value_part(0, 2)
@@ -284,16 +285,18 @@ def tile_picked_yaft_aft_po_kernel(
                 nc.vector.tensor_tensor(result[:, t, :], rr[t][:].indirect(own_sb[:]), mean[t][:], ALU.mult)
 
         rr[0] = leave_bank(2, 0, None)
-        for t in range(PACK):
-            if t + 1 < PACK:
-                rr[t + 1] = leave_bank(2, t + 1, None)
-            gate_on_scalar(t)
-        value_sum(3)
+        rr[1] = leave_bank(2, 1, None)
+        gate_on_scalar(0)
+        rr[2] = leave_bank(2, 2, None)
+        gate_on_scalar(1)
+        rr[3] = leave_bank(2, 3, ACT.Sigmoid)
+        gate_on_scalar(2)
         finish(0)
+        value_sum(3)
         finish(1)
         nc.sync.dma_start(out_rows[:, 0:2, :], result[:, 0:2, :])
-        finish(2)
         finish(3)
+        finish(2)
         nc.sync.dma_start(out_rows[:, 2:4, :], result[:, 2:4, :])
 
         out_grouped = keep.tile([P, V * PACK], BF16, name="out_grouped", align_bytes=64)

@@ -1,6 +1,7 @@
 from contextlib import ExitStack
 
 import concourse.mybir as mybir
+from concourse.masks import make_identity
 
 K, T, S, V, N = 1024, 2048, 512, 256, 512
 FLOPS = 3 * 2 * K * N * S
@@ -26,7 +27,7 @@ PLACE = {
     "raw11": 0, "shares01": 0,
     "lead01": RAW, "lead23": RAW, "mean1": RAW,
     "raw21": 2 * RAW, "part11": 2 * RAW,
-    "x_all1": 3 * RAW, "bias": 3 * RAW,
+    "raw10_0": 3 * RAW, "first0": 3 * RAW, "first1": 3 * RAW + 1024, "first2": 3 * RAW + 2048, "first3": 3 * RAW + 3072,
     "res20": 4 * RAW, "mean3": 4 * RAW,
 }
 
@@ -71,20 +72,24 @@ def tile_picked_yaft_aft_po_kernel(
         nc.vector.memset(warm[:], 0.0)
         warm_out = fresh([P, 1], F32, "warm_out")
         nc.scalar.activation(warm_out[:], warm[:], ACT.Sigmoid)
+        pos_row = fresh([P, 2, V], F32, "pos_row")
+        nc.gpsimd.memset(pos_row[:], 0.0)
+        def load_scales(n):
+            g, r = n % PASSES, n // PASSES
+            nc.sync.dma_start(scale_all[ROWS * g + r : P : 32, :], x_scales[g, r : ROWS * QUADS : ROWS, :].bitcast(I32))
+
         load_weight(0, 0)
         offs_sb = load_list("offs_sb", offs)
+        nc.sync.dma_start(pos_row[0:1, :, :], pos[:, 0:1, :].rearrange("d p v -> p d v"))
+        for n in range(0, 3):
+            load_scales(n)
         x_all = [load_words(0)]
-        for q in range(QUADS):
-            nc.sync.dma_start(
-                scale_all[32 * q : 32 * q + PASSES * ROWS, :],
-                x_scales[:, ROWS * q : ROWS * (q + 1), :].bitcast(I32),
-            )
+        for n in range(3, 8):
+            load_scales(n)
         load_weight(0, 1)
         x_all.append(load_words(1))
         pos1_sb = load_list("pos1_sb", pos1)
         load_weight(1, 0, 0, 64)
-        pos_sb = fresh([P, 2, V], F32, "pos_sb")
-        nc.sync.dma_start(pos_sb[:], pos.rearrange("d p v -> p d v"))
         load_weight(1, 0, 64, P)
         pos2_sb = load_list("pos2_sb", pos2)
         load_weight(1, 1)
@@ -184,6 +189,20 @@ def tile_picked_yaft_aft_po_kernel(
         half_pass(0, 1)
         for t in range(1, PACK):
             one_pass(0, 0, t)
+        ident = fresh([P, P], F32, "ident")
+        make_identity(nc, ident[:])
+        diff_row = fresh([P, V], F32, "diff_row")
+        nc.vector.tensor_tensor(diff_row[:], pos_row[:, 0, :], pos_row[:, 1, :], ALU.subtract)
+        turned = psum.tile([P, 2, P], F32, name="turned", tag="bank11")
+        for i in range(2):
+            nc.tensor.transpose(turned[:, i, :], diff_row[:, i * P : (i + 1) * P], ident[:])
+        diff = fresh([P, 2], F32, "diff")
+        nc.scalar.copy(diff[:], turned[:, :, 0])
+        spread = psum.tile([P, 2, P], F32, name="spread", tag="bank12")
+        for i in range(2):
+            nc.tensor.transpose(spread[:, i, :], diff[:, i : i + 1].to_broadcast([P, P]), ident[:])
+        bias = fresh([P, V], F32, "bias")
+        nc.scalar.copy(bias[:], spread[:].rearrange("p i n -> p (i n)"))
         round_weight(0, 1, nc.scalar, 0, 40)
         round_weight(0, 1, nc.vector, 40, P)
         quantize_weight(0, 1)
@@ -193,8 +212,6 @@ def tile_picked_yaft_aft_po_kernel(
         for t in range(1, PACK):
             one_pass(0, 1, t)
         round_weight(1, 0, nc.vector, 0, 64)
-        bias = fresh([P, V], F32, "bias")
-        nc.vector.tensor_tensor(bias[:], pos_sb[:, 0, :], pos_sb[:, 1, :], ALU.subtract)
 
         kk = [fresh([P, S], F32, "res00")]
         for h in range(2):
@@ -296,7 +313,8 @@ def tile_picked_yaft_aft_po_kernel(
         finish(1)
         nc.sync.dma_start(out_rows[:, 0:2, :], result[:, 0:2, :])
         finish(3)
-        finish(2)
+        for cols in (slice(80, V), slice(0, 80)):
+            nc.vector.tensor_tensor(result[:, 2, cols], gate[2][:, cols], mean[2][:, cols], ALU.mult)
         nc.sync.dma_start(out_rows[:, 2:4, :], result[:, 2:4, :])
 
         out_grouped = keep.tile([P, V * PACK], BF16, name="out_grouped", align_bytes=64)

@@ -23,13 +23,7 @@ PASSES = K // K_PASS
 QUADS = 4
 ROWS = 4
 RAW = PACK * N * 4
-PLACE = {
-    "raw11": 0, "shares01": 0,
-    "lead01": RAW, "lead23": RAW, "mean1": RAW,
-    "raw21": 2 * RAW, "part11": 2 * RAW,
-    "raw10_0": 3 * RAW, "first0": 3 * RAW, "first1": 3 * RAW + 1024, "first2": 3 * RAW + 2048, "first3": 3 * RAW + 3072,
-    "res20": 4 * RAW, "mean3": 4 * RAW,
-}
+PLACE = {"raw21": RAW, "gap0": RAW, "gap2": RAW + 2048, "grouped11": 0, "key13": 0, "raw11": 2 * RAW, "lead1": 2 * RAW, "raw10_0": 3 * RAW, "res02": 3 * RAW, "res03": 3 * RAW + 2048}
 
 
 def tile_picked_yaft_aft_po_kernel(
@@ -74,6 +68,7 @@ def tile_picked_yaft_aft_po_kernel(
         nc.scalar.activation(warm_out[:], warm[:], ACT.Sigmoid)
         pos_row = fresh([P, 2, V], F32, "pos_row")
         nc.gpsimd.memset(pos_row[:], 0.0)
+
         def load_scales(n):
             g, r = n % PASSES, n // PASSES
             nc.sync.dma_start(scale_all[ROWS * g + r : P : 32, :], x_scales[g, r : ROWS * QUADS : ROWS, :].bitcast(I32))
@@ -88,23 +83,20 @@ def tile_picked_yaft_aft_po_kernel(
             load_scales(n)
         load_weight(0, 1)
         x_all.append(load_words(1))
-        pos1_sb = load_list("pos1_sb", pos1)
+        pos2_sb = load_list("pos2_sb", pos2)
         load_weight(1, 0, 0, 64)
         load_weight(1, 0, 64, P)
-        pos2_sb = load_list("pos2_sb", pos2)
+        pos1_sb = load_list("pos1_sb", pos1)
         load_weight(1, 1)
-        for g in range(PASSES):
-            load_weight(2, g)
+        load_weight(2, 0)
+        load_weight(2, 1)
         own_sb = load_list("own_sb", own)
 
         grouped = {}
         codes = {}
         scales = {}
-        grouped_w2 = fresh([P, PASSES * N * PACK], BF16, "grouped_w2")
-        for g in range(PASSES):
-            grouped[1, g] = grouped_w2[:, g * N * PACK : (g + 1) * N * PACK]
 
-        def round_weight(i, g, engine, m0, m1):
+        def round_weight(i, g, engine, m0=0, m1=P):
             if (i, g) not in grouped:
                 grouped[i, g] = fresh([P, N * PACK], BF16, "grouped%d%d" % (i, g))[:]
             dst = grouped[i, g].rearrange("p (h u m j) -> p h m j u", h=2, u=2, j=PACK)[:, :, m0:m1]
@@ -120,13 +112,32 @@ def tile_picked_yaft_aft_po_kernel(
             scales[i, g] = fresh([P, N], U8, "scales%d%d" % (i, g))[:]
             nc.vector.quantize_mx(out=codes[i, g].bitcast(FP8X4), scales=scales[i, g], in_=grouped[i, g])
 
-        def quantize_w2():
-            both_codes = fresh([P, PASSES * N], U32, "codes_w2")
-            both_scales = fresh([P, PASSES * N], U8, "scales_w2")
-            nc.vector.quantize_mx(out=both_codes[:].bitcast(FP8X4), scales=both_scales[:], in_=grouped_w2[:])
-            for g in range(PASSES):
-                codes[1, g] = both_codes[:, g * N : (g + 1) * N]
-                scales[1, g] = both_scales[:, g * N : (g + 1) * N]
+        def round_half(i, g, h, engine=nc.vector):
+            if (i, g) not in grouped:
+                grouped[i, g] = fresh([P, N * PACK], BF16, "grouped%d%d" % (i, g))[:]
+            dst = grouped[i, g].rearrange("p (h u m j) -> p h m j u", h=2, u=2, j=PACK)[:, h]
+            src = raw[i, g][0][2][:].rearrange("p j (m h u) -> p h m j u", h=2, u=2)[:, h]
+            if engine is nc.scalar:
+                nc.scalar.copy(dst, src)
+            else:
+                nc.vector.tensor_copy(dst, src)
+
+        def quantize_half(i, g, h):
+            if (i, g) not in codes:
+                codes[i, g] = fresh([P, N], U32, "codes%d%d" % (i, g))[:]
+                scales[i, g] = fresh([P, N], U8, "scales%d%d" % (i, g))[:]
+            cols = slice(h * N // 2, (h + 1) * N // 2)
+            nc.vector.quantize_mx(
+                out=codes[i, g][:, cols].bitcast(FP8X4),
+                scales=scales[i, g][:, cols],
+                in_=grouped[i, g][:, h * N * 2 : (h + 1) * N * 2],
+            )
+
+        def prepare(i, g):
+            for h in range(2):
+                round_half(i, g, h)
+            for h in range(2):
+                quantize_half(i, g, h)
 
         x_scale = keep.tile([P, S], U8, name="x_scale", align_bytes=64)
         x_code = [keep.tile([P, S], U32, name="x_code%d" % g, align_bytes=64) for g in range(PASSES)]
@@ -136,11 +147,17 @@ def tile_picked_yaft_aft_po_kernel(
                 x_code[g][:, j0:j1], x_all[g][:].bitcast(U32).indirect(offs_sb[:, j0 // 16 : j1 // 16])
             )
 
+        BANK = {
+            (0, 2): 2, (0, 3): 3,
+            (1, 0): 4, (1, 1): 5, (1, 2): 6, (1, 3): 7,
+            (2, 0): 2, (2, 1): 3, (2, 2): 4, (2, 3): 5,
+            "part00": 0, "part01": 7, "part02": 5, "part10": 1, "part11": 6, "bias": 4, "lead0": 0, "share0": 0, "lead2": 1, "share2": 1,
+        }
         banks = {}
 
         def one_pass(i, g, t):
             if g == 0:
-                banks[i, t] = psum.tile([P, S], F32, name="bank%d%d" % (i, t), tag="bank%d%d" % (i % 2, t))
+                banks[i, t] = psum.tile([P, S], F32, name="bank%d%d" % (i, t), tag="bank%d" % BANK[i, t])
             cols = slice(t * P, (t + 1) * P)
             nc.tensor.matmul_mx(
                 out=banks[i, t][:],
@@ -153,17 +170,23 @@ def tile_picked_yaft_aft_po_kernel(
             )
 
         halves = (slice(0, S // 2), slice(S // 2, S))
-        half_banks = [
-            psum.tile([P, S // 2], F32, name="half_bank%d" % h, tag=("bank00", "bank13")[h]) for h in range(2)
-        ]
+        thirds = (slice(0, S // 2), slice(S // 2, 3 * S // 4), slice(3 * S // 4, S))
+        PARTS = (thirds, halves)
+        half_banks = {}
 
-        def half_pass(g, h):
+        def part_pass(g, t, n):
+            part = PARTS[t][n]
+            if g == 0:
+                half_banks[t, n] = psum.tile(
+                    [P, part.stop - part.start], F32, name="part_bank%d%d" % (t, n), tag="bank%d" % BANK["part%d%d" % (t, n)]
+                )
+            cols = slice(t * P, (t + 1) * P)
             nc.tensor.matmul_mx(
-                out=half_banks[h][:],
-                lhsT=codes[0, g][:, 0:P].bitcast(FP8X4),
-                lhsT_scale=scales[0, g][:, 0:P],
-                rhs=x_code[g][:, halves[h]].bitcast(FP8X4),
-                rhs_scale=x_scale[ROWS * g :, halves[h]],
+                out=half_banks[t, n][:],
+                lhsT=codes[0, g][:, cols].bitcast(FP8X4),
+                lhsT_scale=scales[0, g][:, cols],
+                rhs=x_code[g][:, part].bitcast(FP8X4),
+                rhs_scale=x_scale[ROWS * g :, part],
                 start=(g == 0),
                 stop=(g == PASSES - 1),
             )
@@ -172,156 +195,228 @@ def tile_picked_yaft_aft_po_kernel(
             for t in range(PACK):
                 one_pass(i, g, t)
 
-        def leave_bank(i, t, func):
-            tile = fresh([P, S], F32, "res%d%d" % (i, t))
-            if func is None:
-                nc.scalar.copy(tile[:], banks[i, t][:])
+        res = {}
+
+        def leave_bank(i, t, engine=nc.scalar, func=None):
+            res[i, t] = fresh([P, S], F32, "res%d%d" % (i, t))
+            if engine is nc.vector:
+                nc.vector.tensor_copy(res[i, t][:], banks[i, t][:])
+            elif func is None:
+                nc.scalar.copy(res[i, t][:], banks[i, t][:])
             else:
-                nc.scalar.activation(tile[:], banks[i, t][:], func)
-            return tile
+                nc.scalar.activation(res[i, t][:], banks[i, t][:], func)
+
+        ident = fresh([P, P], F32, "ident")
+        make_identity(nc, ident[:])
+        diff_row = fresh([P, V], F32, "diff_row")
+        nc.vector.tensor_tensor(diff_row[:], pos_row[:, 0, :], pos_row[:, 1, :], ALU.subtract)
+        turned = psum.tile([P, 2, P], F32, name="turned", tag="bank%d" % BANK["bias"])
+        for c in range(2):
+            nc.tensor.transpose(turned[:, c, :], diff_row[:, c * P : (c + 1) * P], ident[:])
+        bias = fresh([P, 2], F32, "bias")
+        nc.scalar.copy(bias[:], turned[:, :, 0])
 
         round_weight(0, 0, nc.scalar, 0, 48)
         round_weight(0, 0, nc.vector, 48, P)
         quantize_weight(0, 0)
         gather_words(0)
         nc.vector.tensor_copy(x_scale[:], scale_all[:].bitcast(U8).indirect(offs_sb[:]))
-        half_pass(0, 0)
-        half_pass(0, 1)
-        for t in range(1, PACK):
+        for t in range(2):
+            for n in range(len(PARTS[t])):
+                part_pass(0, t, n)
+        for t in range(2, PACK):
             one_pass(0, 0, t)
-        ident = fresh([P, P], F32, "ident")
-        make_identity(nc, ident[:])
-        diff_row = fresh([P, V], F32, "diff_row")
-        nc.vector.tensor_tensor(diff_row[:], pos_row[:, 0, :], pos_row[:, 1, :], ALU.subtract)
-        turned = psum.tile([P, 2, P], F32, name="turned", tag="bank11")
-        for i in range(2):
-            nc.tensor.transpose(turned[:, i, :], diff_row[:, i * P : (i + 1) * P], ident[:])
-        diff = fresh([P, 2], F32, "diff")
-        nc.scalar.copy(diff[:], turned[:, :, 0])
-        spread = psum.tile([P, 2, P], F32, name="spread", tag="bank12")
-        for i in range(2):
-            nc.tensor.transpose(spread[:, i, :], diff[:, i : i + 1].to_broadcast([P, P]), ident[:])
-        bias = fresh([P, V], F32, "bias")
-        nc.scalar.copy(bias[:], spread[:].rearrange("p i n -> p (i n)"))
         round_weight(0, 1, nc.scalar, 0, 40)
         round_weight(0, 1, nc.vector, 40, P)
         quantize_weight(0, 1)
-        for h in range(2):
-            gather_words(1, halves[h].start, halves[h].stop)
-            half_pass(1, h)
-        for t in range(1, PACK):
+        for n in range(3):
+            gather_words(1, thirds[n].start, thirds[n].stop)
+            part_pass(1, 0, n)
+            if n != 1:
+                part_pass(1, 1, n // 2)
+        for t in range(2, PACK):
             one_pass(0, 1, t)
-        round_weight(1, 0, nc.vector, 0, 64)
 
-        kk = [fresh([P, S], F32, "res00")]
-        for h in range(2):
-            nc.scalar.copy(kk[0][:, halves[h]], half_banks[h][:])
-        kk.extend(leave_bank(0, t, None) for t in range(1, PACK))
-        first, lead, share = {}, {}, {}
-        signs = (-1.0, 1.0)
-        lead_pair = {0: fresh([P, 2, V], F32, "lead01"), 2: fresh([P, 2, V], F32, "lead23")}
+        for t in range(2):
+            res[0, t] = fresh([P, S], F32, "res0%d" % t)
+        for n in range(3):
+            nc.scalar.copy(res[0, 0][:, thirds[n]], half_banks[0, n][:])
 
-        def key_first(t):
-            first[t] = fresh([P, V], F32, "first%d" % t)
-            nc.vector.tensor_tensor(first[t][:], kk[t][:].indirect(pos1_sb[:]), bias[:], ALU.add)
+        terms = {}
+        picked, lead_bank, share_rows, share_bank = {}, {}, {}, {}
+        second, gap, step, mean, gate = {}, {}, {}, {}, {}
+
+        def pair(store, t, name):
+            t0 = t - t % 2
+            if t0 not in store:
+                store[t0] = fresh([P, 2, V], F32, "%s%d" % (name, t0))
+            return store[t0][:, t % 2, :]
+
+        def key_plain(t, offsets, name, sign=1.0):
+            picked[name, t] = fresh([P, V], F32, "%s%d" % (name, t))
+            if sign == 1.0:
+                nc.scalar.activation(picked[name, t][:], res[0, t][:].indirect(offsets[:]), ACT.Copy)
+            else:
+                nc.scalar.activation(picked[name, t][:], res[0, t][:].indirect(offsets[:]), ACT.Copy, scale=sign)
 
         def key_second(t):
+            key_plain(t, pos2_sb, "key2")
+
+        def spent(i, g):
+            return raw[i, g][0][2][:, 0:2, 0:V]
+
+        def round_halves(i, g):
+            round_weight(i, g, nc.vector, 0, P // 2)
+            round_weight(i, g, nc.vector, P // 2, P)
+
+        def key_lead(t, target=None):
+            picked["lead", t] = fresh([P, V], F32, "lead%d" % t)[:] if target is None else target
             nc.vector.tensor_tensor(
-                lead_pair[t - t % 2][:, t % 2, :], kk[t][:].indirect(pos2_sb[:]), first[t][:], ALU.subtract
+                picked["lead", t], res[0, t][:].indirect(pos1_sb[:]), picked["key2", t][:], ALU.subtract
             )
+            terms[t] = [picked["lead", t]]
+
+        def key_both(t):
+            key_plain(t, pos1_sb, "key1")
+            key_plain(t, pos2_sb, "key2", -1.0)
+            terms[t] = [picked["key1", t], picked["key2", t]]
+
+        def turn_leads(t0):
+            lead_bank[t0] = psum.tile([P, 2, 2, P], F32, name="lead_bank%d" % t0, tag="bank%d" % BANK["lead%d" % t0])
+            for u in (1, 0):
+                for c in range(2):
+                    for n, term in enumerate(terms[t0 + u]):
+                        nc.tensor.matmul(
+                            lead_bank[t0][:, c, u, :],
+                            lhsT=term[:, c * P : (c + 1) * P],
+                            rhs=ident[:],
+                            is_transpose=True,
+                            start=(n == 0),
+                            stop=(n == len(terms[t0 + u]) - 1),
+                        )
 
         def shares(t0):
-            both = fresh([P, 2, 2, V], F32, "shares%d%d" % (t0, t0 + 1))
-            for d in range(2):
-                nc.scalar.activation(both[:, d, :, :], lead_pair[t0][:], ACT.Sigmoid, scale=signs[d])
-                share[d, t0], share[d, t0 + 1] = both[:, d, 0, :], both[:, d, 1, :]
+            share_rows[t0] = fresh([P, 2, 2, P], F32, "share_rows%d" % t0)
+            for c in range(2):
+                nc.scalar.activation(
+                    share_rows[t0][:, c, :, :], lead_bank[t0][:, c, :, :], ACT.Sigmoid, bias=bias[:, c : c + 1]
+                )
 
-        part, mean, vv, gate, rr = {}, {}, {}, {}, {}
-        lists = (pos1_sb, pos2_sb)
+        def turn_back(t0):
+            share_bank[t0] = psum.tile([P, 2, V], F32, name="share_bank%d" % t0, tag="bank%d" % BANK["share%d" % t0])
+            for u in range(2):
+                for c in range(2):
+                    nc.tensor.transpose(share_bank[t0][:, u, c * P : (c + 1) * P], share_rows[t0][:, c, u, :], ident[:])
 
-        def value_part(d, t):
-            part[d, t] = fresh([P, V], F32, "part%d%d" % (d, t))
-            nc.vector.tensor_tensor(part[d, t][:], vv[t][:].indirect(lists[d][:]), share[d, t], ALU.mult)
+        def value_second(t, engine=nc.scalar):
+            if engine is nc.scalar:
+                nc.scalar.activation(pair(second, t, "second"), res[1, t][:].indirect(pos2_sb[:]), ACT.Copy)
+            else:
+                nc.vector.tensor_copy(pair(second, t, "second"), res[1, t][:].indirect(pos2_sb[:]))
 
-        def value_sum(t):
-            mean[t] = fresh([P, V], F32, "mean%d" % t)
-            nc.vector.tensor_tensor(mean[t][:], part[0, t][:], part[1, t][:], ALU.add)
+        def value_gap(t):
+            nc.vector.tensor_tensor(
+                pair(gap, t, "gap"), res[1, t][:].indirect(pos1_sb[:]), pair(second, t, "second"), ALU.subtract
+            )
 
-        key_first(0)
-        round_weight(1, 0, nc.scalar, 64, P)
-        round_weight(1, 1, nc.scalar, 0, 96)
-        key_first(1)
-        key_second(0)
-        key_first(2)
-        key_second(1)
-        key_first(3)
-        round_weight(1, 1, nc.vector, 96, P)
-        quantize_w2()
-        for t in range(PACK):
-            for g in range(PASSES):
-                one_pass(1, g, t)
-        shares(0)
-        round_weight(2, 0, nc.scalar, 0, 84)
-        key_second(2)
-        key_second(3)
-        round_weight(2, 0, nc.vector, 84, P)
-        vv[0] = leave_bank(1, 0, None)
-        vv[1] = leave_bank(1, 1, None)
-        round_weight(2, 1, nc.vector, 72, P)
-        quantize_weight(2, 0)
-        multiply(2, 0)
-        round_weight(2, 1, nc.scalar, 0, 72)
-        value_part(0, 0)
-        value_part(1, 0)
-        value_part(0, 1)
-        value_sum(0)
-        quantize_weight(2, 1)
-        multiply(2, 1)
-        vv[2] = leave_bank(1, 2, None)
-        shares(2)
-        vv[3] = leave_bank(1, 3, None)
-        value_part(1, 1)
-        value_part(0, 2)
-        value_sum(1)
-        value_part(1, 2)
-        value_part(0, 3)
-        value_sum(2)
-        value_part(1, 3)
+        def value_step(t0):
+            step[t0] = fresh([P, 2, V], F32, "step%d" % t0)
+            nc.vector.tensor_tensor(step[t0][:], gap[t0][:], share_bank[t0][:], ALU.mult)
+
+        def value_mean(t0):
+            mean[t0] = fresh([P, 2, V], F32, "mean%d" % t0)
+            nc.vector.tensor_tensor(mean[t0][:], step[t0][:], second[t0][:], ALU.add)
 
         result = keep.tile([P, PACK, V], F32, name="result")
         out_rows = out_0.rearrange("(p t) v -> p t v", t=PACK)
 
         def gate_on_scalar(t):
-            gate[t] = fresh([P, V], F32, "gate%d" % t)
-            nc.scalar.activation(gate[t][:], rr[t][:].indirect(own_sb[:]), ACT.Sigmoid)
+            nc.scalar.activation(pair(gate, t, "gate"), res[2, t][:].indirect(own_sb[:]), ACT.Sigmoid)
 
-        def finish(t):
-            if t in gate:
-                nc.vector.tensor_tensor(result[:, t, :], gate[t][:], mean[t][:], ALU.mult)
-            else:
-                nc.vector.tensor_tensor(result[:, t, :], rr[t][:].indirect(own_sb[:]), mean[t][:], ALU.mult)
+        def finish_pair(t0):
+            nc.vector.tensor_tensor(result[:, t0 : t0 + 2, :], gate[t0][:], mean[t0][:], ALU.mult)
 
-        rr[0] = leave_bank(2, 0, None)
-        rr[1] = leave_bank(2, 1, None)
-        gate_on_scalar(0)
-        rr[2] = leave_bank(2, 2, None)
-        gate_on_scalar(1)
-        rr[3] = leave_bank(2, 3, ACT.Sigmoid)
+        def finish_gated(t):
+            nc.vector.tensor_tensor(result[:, t, :], pair(gate, t, "gate"), pair(mean, t, "mean"), ALU.mult)
+
+        def finish(t, v0=0, v1=V):
+            nc.vector.tensor_tensor(
+                result[:, t, v0:v1],
+                res[2, t][:].indirect(own_sb[:, v0 // 16 : v1 // 16]),
+                pair(mean, t, "mean")[:, v0:v1],
+                ALU.mult,
+            )
+
+        def store(t0, t1):
+            nc.sync.dma_start(out_rows[:, t0:t1, :], result[:, t0:t1, :])
+
+        nc.vector.tensor_copy(res[0, 1][:, halves[0]], half_banks[1, 0][:])
+        round_weight(1, 0, nc.vector, 0, 64)
+        nc.vector.tensor_copy(res[0, 1][:, halves[1]], half_banks[1, 1][:])
+        key_second(0)
+        round_weight(1, 0, nc.vector, 64, P)
+        key_lead(0)
+        quantize_weight(1, 0)
+        multiply(1, 0)
+        leave_bank(0, 2)
+        leave_bank(0, 3)
+        key_second(1)
+        prepare(1, 1)
+        multiply(1, 1)
+        key_lead(1)
+        turn_leads(0)
+        key_plain(2, pos2_sb, "key2", -1.0)
+        key_plain(3, pos2_sb, "key2", -1.0)
+        key_plain(2, pos1_sb, "key1")
+        key_plain(3, pos1_sb, "key1")
+        terms[2] = [picked["key1", 2], picked["key2", 2]]
+        terms[3] = [picked["key1", 3], picked["key2", 3]]
+        turn_leads(2)
+        prepare(2, 0)
+        leave_bank(1, 0)
+        leave_bank(1, 1)
+        value_second(0)
+        value_second(1)
+        multiply(2, 0)
+        shares(0)
+        turn_back(0)
+        shares(2)
+        turn_back(2)
+        round_half(2, 1, 0)
+        round_half(2, 1, 1)
+        quantize_half(2, 1, 0)
+        value_gap(0)
+        value_gap(1)
+        quantize_half(2, 1, 1)
+        multiply(2, 1)
+        leave_bank(1, 2)
+        leave_bank(1, 3)
+        value_second(2)
+        value_second(3)
+        value_step(0)
+        value_gap(2)
+        value_gap(3)
+        value_mean(0)
+        value_step(2)
+        leave_bank(2, 0, func=ACT.Sigmoid)
+        leave_bank(2, 1, func=ACT.Sigmoid)
+        leave_bank(2, 2)
+        leave_bank(2, 3)
         gate_on_scalar(2)
+        gate_on_scalar(3)
         finish(0)
-        value_sum(3)
+        value_mean(2)
         finish(1)
-        nc.sync.dma_start(out_rows[:, 0:2, :], result[:, 0:2, :])
-        finish(3)
-        for cols in (slice(80, V), slice(0, 80)):
-            nc.vector.tensor_tensor(result[:, 2, cols], gate[2][:, cols], mean[2][:, cols], ALU.mult)
-        nc.sync.dma_start(out_rows[:, 2:4, :], result[:, 2:4, :])
+        store(0, 2)
+        for cols in (slice(0, 160), slice(160, V)):
+            nc.vector.tensor_tensor(result[:, 2:4, cols], gate[2][:, :, cols], mean[2][:, :, cols], ALU.mult)
+        store(2, 4)
 
         out_grouped = keep.tile([P, V * PACK], BF16, name="out_grouped", align_bytes=64)
         dst = out_grouped[:].rearrange("p (c i t) -> p c t i", i=4, t=PACK)
         src = result[:].rearrange("p t (c i) -> p c t i", i=4)
-        nc.vector.tensor_copy(dst[:, 20:], src[:, 20:])
-        nc.scalar.copy(dst[:, :20], src[:, :20])
+        nc.scalar.copy(dst[:, :40], src[:, :40])
+        nc.vector.tensor_copy(dst[:, 40:], src[:, 40:])
         out_codes = keep.tile([P, V], U32, name="out_codes", align_bytes=64)
         out_scales = keep.tile([P, V], U8, name="out_scales", align_bytes=64)
         nc.vector.quantize_mx(out=out_codes[:].bitcast(FP8X4), scales=out_scales[:], in_=out_grouped[:])

@@ -23,7 +23,7 @@ PASSES = K // K_PASS
 QUADS = 4
 ROWS = 4
 RAW = PACK * N * 4
-PLACE = {"raw21": RAW, "gap0": RAW, "gap2": RAW + 2048, "grouped11": 0, "key13": 0, "raw11": 2 * RAW, "lead1": 2 * RAW, "raw10_0": 3 * RAW, "res02": 3 * RAW, "res03": 3 * RAW + 2048}
+PLACE = {"raw21": RAW, "gap0": RAW, "gap2": RAW + 2048, "grouped11": 0, "raw10_64": 0}
 
 
 def tile_picked_yaft_aft_po_kernel(
@@ -85,8 +85,8 @@ def tile_picked_yaft_aft_po_kernel(
         x_all.append(load_words(1))
         pos2_sb = load_list("pos2_sb", pos2)
         load_weight(1, 0, 0, 64)
-        load_weight(1, 0, 64, P)
         pos1_sb = load_list("pos1_sb", pos1)
+        load_weight(1, 0, 64, P)
         load_weight(1, 1)
         load_weight(2, 0)
         load_weight(2, 1)
@@ -104,6 +104,10 @@ def tile_picked_yaft_aft_po_kernel(
             src = tile[:].rearrange("p j (m h u) -> p h m j u", h=2, u=2)[:, :, m0 - start : m1 - start]
             if engine is nc.scalar:
                 nc.scalar.copy(dst, src)
+            elif engine is nc.gpsimd:
+                dst = grouped[i, g].rearrange("p (t m j) -> p m t j", t=PACK, j=PACK)[:, m0:m1]
+                src = tile[:].rearrange("p j (m t) -> p m t j", t=PACK)[:, m0 - start : m1 - start]
+                nc.gpsimd.tensor_scalar(dst, src, 1.0, 0.0, ALU.mult, ALU.add)
             else:
                 nc.vector.tensor_copy(dst, src)
 
@@ -148,10 +152,10 @@ def tile_picked_yaft_aft_po_kernel(
             )
 
         BANK = {
-            (0, 2): 2, (0, 3): 3,
+            (0, 2): 2, (0, 3): 6,
             (1, 0): 4, (1, 1): 5, (1, 2): 6, (1, 3): 7,
-            (2, 0): 2, (2, 1): 3, (2, 2): 4, (2, 3): 5,
-            "part00": 0, "part01": 7, "part02": 5, "part10": 1, "part11": 6, "bias": 4, "lead0": 0, "share0": 0, "lead2": 1, "share2": 1,
+            (2, 0): 2, (2, 1): 3, (2, 2): 1, (2, 3): 0,
+            "part00": 0, "part01": 7, "part02": 5, "part10": 1, "part11": 6, "bias": 4, "lead0": 0, "share0": 5, "lead2": 4, "share2": 4,
         }
         banks = {}
 
@@ -224,8 +228,7 @@ def tile_picked_yaft_aft_po_kernel(
         for t in range(2):
             for n in range(len(PARTS[t])):
                 part_pass(0, t, n)
-        for t in range(2, PACK):
-            one_pass(0, 0, t)
+        one_pass(0, 0, 2)
         round_weight(0, 1, nc.scalar, 0, 40)
         round_weight(0, 1, nc.vector, 40, P)
         quantize_weight(0, 1)
@@ -234,8 +237,7 @@ def tile_picked_yaft_aft_po_kernel(
             part_pass(1, 0, n)
             if n != 1:
                 part_pass(1, 1, n // 2)
-        for t in range(2, PACK):
-            one_pass(0, 1, t)
+        one_pass(0, 1, 2)
 
         for t in range(2):
             res[0, t] = fresh([P, S], F32, "res0%d" % t)
@@ -350,36 +352,40 @@ def tile_picked_yaft_aft_po_kernel(
         def store(t0, t1):
             nc.sync.dma_start(out_rows[:, t0:t1, :], result[:, t0:t1, :])
 
-        nc.vector.tensor_copy(res[0, 1][:, halves[0]], half_banks[1, 0][:])
-        round_weight(1, 0, nc.vector, 0, 64)
-        nc.vector.tensor_copy(res[0, 1][:, halves[1]], half_banks[1, 1][:])
-        key_second(0)
-        round_weight(1, 0, nc.vector, 64, P)
-        key_lead(0)
+        def key_on_vector(t):
+            picked["key1", t] = fresh([P, V], F32, "key1%d" % t)
+            nc.vector.tensor_copy(picked["key1", t][:], res[0, t][:].indirect(pos1_sb[:]))
+
+        round_weight(1, 0, nc.gpsimd, 0, 64)
+        round_weight(1, 0, nc.gpsimd, 64, P)
+        for n in range(2):
+            nc.vector.tensor_copy(res[0, 1][:, halves[n]], half_banks[1, n][:])
+        for g in range(PASSES):
+            one_pass(0, g, 3)
+        for t in range(2):
+            key_plain(t, pos2_sb, "key2", -1.0)
+            key_on_vector(t)
+        leave_bank(0, 3)
+        leave_bank(0, 2, nc.vector)
+        for t in (3, 2):
+            key_plain(t, pos2_sb, "key2", -1.0)
+            key_plain(t, pos1_sb, "key1")
+        for t in range(PACK):
+            terms[t] = [picked["key1", t], picked["key2", t]]
+        turn_leads(0)
         quantize_weight(1, 0)
         multiply(1, 0)
-        leave_bank(0, 2)
-        leave_bank(0, 3)
-        key_second(1)
         prepare(1, 1)
         multiply(1, 1)
-        key_lead(1)
-        turn_leads(0)
-        key_plain(2, pos2_sb, "key2", -1.0)
-        key_plain(3, pos2_sb, "key2", -1.0)
-        key_plain(2, pos1_sb, "key1")
-        key_plain(3, pos1_sb, "key1")
-        terms[2] = [picked["key1", 2], picked["key2", 2]]
-        terms[3] = [picked["key1", 3], picked["key2", 3]]
-        turn_leads(2)
         prepare(2, 0)
+        shares(0)
         leave_bank(1, 0)
         leave_bank(1, 1)
+        turn_leads(2)
+        turn_back(0)
         value_second(0)
         value_second(1)
         multiply(2, 0)
-        shares(0)
-        turn_back(0)
         shares(2)
         turn_back(2)
         round_half(2, 1, 0)

@@ -414,15 +414,20 @@ def tile_picked_yaft_aft_po_kernel(
         value_mean(2)
         finish(1)
         store(0, 2)
-        for cols in (slice(0, 160), slice(160, V)):
+        pieces = (slice(0, 96), slice(96, 176), slice(176, V))
+        for cols in pieces:
             nc.vector.tensor_tensor(result[:, 2:4, cols], gate[2][:, :, cols], mean[2][:, :, cols], ALU.mult)
         store(2, 4)
 
         out_grouped = keep.tile([P, V * PACK], BF16, name="out_grouped", align_bytes=64)
         dst = out_grouped[:].rearrange("p (c i t) -> p c t i", i=4, t=PACK)
         src = result[:].rearrange("p t (c i) -> p c t i", i=4)
-        nc.scalar.copy(dst[:, :40], src[:, :40])
-        nc.vector.tensor_copy(dst[:, 40:], src[:, 40:])
+        for n, cols in enumerate(pieces):
+            runs = slice(cols.start // 4, cols.stop // 4)
+            if n == 0:
+                nc.scalar.copy(dst[:, runs], src[:, runs])
+            else:
+                nc.vector.tensor_copy(dst[:, runs], src[:, runs])
         out_codes = keep.tile([P, V], U32, name="out_codes", align_bytes=64)
         out_scales = keep.tile([P, V], U8, name="out_scales", align_bytes=64)
         nc.vector.quantize_mx(out=out_codes[:].bitcast(FP8X4), scales=out_scales[:], in_=out_grouped[:])

@@ -411,13 +411,16 @@ def tile_picked_yaft_aft_po_kernel(
         gate_on_scalar(2)
         gate_on_scalar(3)
         finish(0)
+        store(0, 1)
         value_mean(2)
         finish(1)
-        store(0, 2)
+        store(1, 2)
+        finish_gated(2)
+        store(2, 3)
         pieces = (slice(0, 96), slice(96, 176), slice(176, V))
         for cols in pieces:
-            nc.vector.tensor_tensor(result[:, 2:4, cols], gate[2][:, :, cols], mean[2][:, :, cols], ALU.mult)
-        store(2, 4)
+            nc.vector.tensor_tensor(result[:, 3, cols], gate[2][:, 1, cols], mean[2][:, 1, cols], ALU.mult)
+        store(3, 4)
 
         out_grouped = keep.tile([P, V * PACK], BF16, name="out_grouped", align_bytes=64)
         dst = out_grouped[:].rearrange("p (c i t) -> p c t i", i=4, t=PACK)

from contextlib import ExitStack

import concourse.mybir as mybir
from concourse.masks import make_identity

K, T, S, V, N = 1024, 2048, 512, 256, 512
FLOPS = 3 * 2 * K * N * S

F32 = mybir.dt.float32
BF16 = mybir.dt.bfloat16
I32 = mybir.dt.int32
U32 = mybir.dt.uint32
U16 = mybir.dt.uint16
U8 = mybir.dt.uint8
FP8X4 = mybir.dt.float8_e4m3fn_x4
ALU = mybir.AluOpType
ACT = mybir.ActivationFunctionType

P = 128
PACK = 4
K_PASS = P * PACK
PASSES = K // K_PASS
QUADS = 4
ROWS = 4
RAW = PACK * N * 4
PLACE = {"raw21": RAW, "gap0": RAW, "gap2": RAW + 2048, "grouped11": 0, "raw10_64": 0}


def tile_picked_yaft_aft_po_kernel(
    tc, x_words, x_scales, w1, w2, w3, pos, offs, pos1, pos2, own, out_0, out_1, out_2
):
    nc = tc.nc
    weights = (w1, w2, w3)
    with ExitStack() as ctx:
        keep = ctx.enter_context(tc.tile_pool(name="keep", bufs=1))
        arena = ctx.enter_context(tc.tile_pool(name="arena", bufs=1))
        psum = ctx.enter_context(tc.psum_pool(name="psum", bufs=1))

        def fresh(shape, dtype, name):
            if name in PLACE:
                return arena.tile(shape, dtype, name=name, offset=PLACE[name], align_bytes=64)
            return keep.tile(shape, dtype, name=name, align_bytes=64)

        def load_list(name, src):
            tile = keep.tile(list(src.shape), U16, name=name)
            nc.sync.dma_start(tile[:], src)
            return tile

        raw = {}

        def load_weight(i, g, m0=0, m1=P):
            name = "raw%d%d" % (i, g) if m1 - m0 == P else "raw%d%d_%d" % (i, g, m0)
            tile = fresh([P, PACK, PACK * (m1 - m0)], F32, name)
            rows = weights[i][g * K_PASS : (g + 1) * K_PASS, PACK * m0 : PACK * m1]
            nc.sync.dma_start(tile[:], rows.rearrange("(p j) c -> p j c", j=PACK))
            raw.setdefault((i, g), []).append((m0, m1, tile))

        def load_words(g):
            tile = fresh([P, T], I32, "x_all%d" % g)
            nc.sync.dma_start(tile[:], x_words[g].rearrange("p n t -> p (n t)").bitcast(I32))
            return tile

        scale_all = fresh([P, T // 4], I32, "scale_all")
        nc.vector.memset(scale_all[:], 0)
        warm = fresh([P, 1], F32, "warm_in")
        nc.vector.memset(warm[:], 0.0)
        warm_out = fresh([P, 1], F32, "warm_out")
        nc.scalar.activation(warm_out[:], warm[:], ACT.Sigmoid)
        pos_row = fresh([P, 2, V], F32, "pos_row")
        nc.gpsimd.memset(pos_row[:], 0.0)

        def load_scales(n):
            g, r = n % PASSES, n // PASSES
            nc.sync.dma_start(scale_all[ROWS * g + r : P : 32, :], x_scales[g, r : ROWS * QUADS : ROWS, :].bitcast(I32))

        load_weight(0, 0)
        offs_sb = load_list("offs_sb", offs)
        nc.sync.dma_start(pos_row[0:1, :, :], pos[:, 0:1, :].rearrange("d p v -> p d v"))
        for n in range(0, 3):
            load_scales(n)
        x_all = [load_words(0)]
        for n in range(3, 8):
            load_scales(n)
        load_weight(0, 1)
        x_all.append(load_words(1))
        pos2_sb = load_list("pos2_sb", pos2)
        load_weight(1, 0, 0, 64)
        pos1_sb = load_list("pos1_sb", pos1)
        load_weight(1, 0, 64, P)
        load_weight(1, 1)
        load_weight(2, 0)
        load_weight(2, 1)
        own_sb = load_list("own_sb", own)

        grouped = {}
        codes = {}
        scales = {}

        def round_weight(i, g, engine, m0=0, m1=P):
            if (i, g) not in grouped:
                grouped[i, g] = fresh([P, N * PACK], BF16, "grouped%d%d" % (i, g))[:]
            dst = grouped[i, g].rearrange("p (h u m j) -> p h m j u", h=2, u=2, j=PACK)[:, :, m0:m1]
            start, tile = [(a, tile) for a, b, tile in raw[i, g] if a <= m0 and m1 <= b][0]
            src = tile[:].rearrange("p j (m h u) -> p h m j u", h=2, u=2)[:, :, m0 - start : m1 - start]
            if engine is nc.scalar:
                nc.scalar.copy(dst, src)
            elif engine is nc.gpsimd:
                dst = grouped[i, g].rearrange("p (t m j) -> p m t j", t=PACK, j=PACK)[:, m0:m1]
                src = tile[:].rearrange("p j (m t) -> p m t j", t=PACK)[:, m0 - start : m1 - start]
                nc.gpsimd.tensor_scalar(dst, src, 1.0, 0.0, ALU.mult, ALU.add)
            else:
                nc.vector.tensor_copy(dst, src)

        def quantize_weight(i, g):
            codes[i, g] = fresh([P, N], U32, "codes%d%d" % (i, g))[:]
            scales[i, g] = fresh([P, N], U8, "scales%d%d" % (i, g))[:]
            nc.vector.quantize_mx(out=codes[i, g].bitcast(FP8X4), scales=scales[i, g], in_=grouped[i, g])

        def round_half(i, g, h, engine=nc.vector):
            if (i, g) not in grouped:
                grouped[i, g] = fresh([P, N * PACK], BF16, "grouped%d%d" % (i, g))[:]
            dst = grouped[i, g].rearrange("p (h u m j) -> p h m j u", h=2, u=2, j=PACK)[:, h]
            src = raw[i, g][0][2][:].rearrange("p j (m h u) -> p h m j u", h=2, u=2)[:, h]
            if engine is nc.scalar:
                nc.scalar.copy(dst, src)
            else:
                nc.vector.tensor_copy(dst, src)

        def quantize_half(i, g, h):
            if (i, g) not in codes:
                codes[i, g] = fresh([P, N], U32, "codes%d%d" % (i, g))[:]
                scales[i, g] = fresh([P, N], U8, "scales%d%d" % (i, g))[:]
            cols = slice(h * N // 2, (h + 1) * N // 2)
            nc.vector.quantize_mx(
                out=codes[i, g][:, cols].bitcast(FP8X4),
                scales=scales[i, g][:, cols],
                in_=grouped[i, g][:, h * N * 2 : (h + 1) * N * 2],
            )

        def prepare(i, g):
            for h in range(2):
                round_half(i, g, h)
            for h in range(2):
                quantize_half(i, g, h)

        x_scale = keep.tile([P, S], U8, name="x_scale", align_bytes=64)
        x_code = [keep.tile([P, S], U32, name="x_code%d" % g, align_bytes=64) for g in range(PASSES)]

        def gather_words(g, j0=0, j1=S):
            nc.vector.tensor_copy(
                x_code[g][:, j0:j1], x_all[g][:].bitcast(U32).indirect(offs_sb[:, j0 // 16 : j1 // 16])
            )

        BANK = {
            (0, 2): 2, (0, 3): 6,
            (1, 0): 4, (1, 1): 5, (1, 2): 6, (1, 3): 7,
            (2, 0): 2, (2, 1): 3, (2, 2): 1, (2, 3): 0,
            "part00": 0, "part01": 7, "part02": 5, "part10": 1, "part11": 6, "bias": 4, "lead0": 0, "share0": 5, "lead2": 4, "share2": 4,
        }
        banks = {}

        def one_pass(i, g, t):
            if g == 0:
                banks[i, t] = psum.tile([P, S], F32, name="bank%d%d" % (i, t), tag="bank%d" % BANK[i, t])
            cols = slice(t * P, (t + 1) * P)
            nc.tensor.matmul_mx(
                out=banks[i, t][:],
                lhsT=codes[i, g][:, cols].bitcast(FP8X4),
                lhsT_scale=scales[i, g][:, cols],
                rhs=x_code[g][:].bitcast(FP8X4),
                rhs_scale=x_scale[ROWS * g :, :],
                start=(g == 0),
                stop=(g == PASSES - 1),
            )

        halves = (slice(0, S // 2), slice(S // 2, S))
        thirds = (slice(0, S // 2), slice(S // 2, 3 * S // 4), slice(3 * S // 4, S))
        PARTS = (thirds, halves)
        half_banks = {}

        def part_pass(g, t, n):
            part = PARTS[t][n]
            if g == 0:
                half_banks[t, n] = psum.tile(
                    [P, part.stop - part.start], F32, name="part_bank%d%d" % (t, n), tag="bank%d" % BANK["part%d%d" % (t, n)]
                )
            cols = slice(t * P, (t + 1) * P)
            nc.tensor.matmul_mx(
                out=half_banks[t, n][:],
                lhsT=codes[0, g][:, cols].bitcast(FP8X4),
                lhsT_scale=scales[0, g][:, cols],
                rhs=x_code[g][:, part].bitcast(FP8X4),
                rhs_scale=x_scale[ROWS * g :, part],
                start=(g == 0),
                stop=(g == PASSES - 1),
            )

        def multiply(i, g):
            for t in range(PACK):
                one_pass(i, g, t)

        res = {}

        def leave_bank(i, t, engine=nc.scalar, func=None):
            res[i, t] = fresh([P, S], F32, "res%d%d" % (i, t))
            if engine is nc.vector:
                nc.vector.tensor_copy(res[i, t][:], banks[i, t][:])
            elif func is None:
                nc.scalar.copy(res[i, t][:], banks[i, t][:])
            else:
                nc.scalar.activation(res[i, t][:], banks[i, t][:], func)

        ident = fresh([P, P], F32, "ident")
        make_identity(nc, ident[:])
        diff_row = fresh([P, V], F32, "diff_row")
        nc.vector.tensor_tensor(diff_row[:], pos_row[:, 0, :], pos_row[:, 1, :], ALU.subtract)
        turned = psum.tile([P, 2, P], F32, name="turned", tag="bank%d" % BANK["bias"])
        for c in range(2):
            nc.tensor.transpose(turned[:, c, :], diff_row[:, c * P : (c + 1) * P], ident[:])
        bias = fresh([P, 2], F32, "bias")
        nc.scalar.copy(bias[:], turned[:, :, 0])

        round_weight(0, 0, nc.scalar, 0, 48)
        round_weight(0, 0, nc.vector, 48, P)
        quantize_weight(0, 0)
        gather_words(0)
        nc.vector.tensor_copy(x_scale[:], scale_all[:].bitcast(U8).indirect(offs_sb[:]))
        for t in range(2):
            for n in range(len(PARTS[t])):
                part_pass(0, t, n)
        one_pass(0, 0, 2)
        round_weight(0, 1, nc.scalar, 0, 40)
        round_weight(0, 1, nc.vector, 40, P)
        quantize_weight(0, 1)
        for n in range(3):
            gather_words(1, thirds[n].start, thirds[n].stop)
            part_pass(1, 0, n)
            if n != 1:
                part_pass(1, 1, n // 2)
        one_pass(0, 1, 2)

        for t in range(2):
            res[0, t] = fresh([P, S], F32, "res0%d" % t)
        for n in range(3):
            nc.scalar.copy(res[0, 0][:, thirds[n]], half_banks[0, n][:])

        terms = {}
        picked, lead_bank, share_rows, share_bank = {}, {}, {}, {}
        second, gap, step, mean, gate = {}, {}, {}, {}, {}

        def pair(store, t, name):
            t0 = t - t % 2
            if t0 not in store:
                store[t0] = fresh([P, 2, V], F32, "%s%d" % (name, t0))
            return store[t0][:, t % 2, :]

        def key_plain(t, offsets, name, sign=1.0):
            picked[name, t] = fresh([P, V], F32, "%s%d" % (name, t))
            if sign == 1.0:
                nc.scalar.activation(picked[name, t][:], res[0, t][:].indirect(offsets[:]), ACT.Copy)
            else:
                nc.scalar.activation(picked[name, t][:], res[0, t][:].indirect(offsets[:]), ACT.Copy, scale=sign)

        def key_second(t):
            key_plain(t, pos2_sb, "key2")

        def spent(i, g):
            return raw[i, g][0][2][:, 0:2, 0:V]

        def round_halves(i, g):
            round_weight(i, g, nc.vector, 0, P // 2)
            round_weight(i, g, nc.vector, P // 2, P)

        def key_lead(t, target=None):
            picked["lead", t] = fresh([P, V], F32, "lead%d" % t)[:] if target is None else target
            nc.vector.tensor_tensor(
                picked["lead", t], res[0, t][:].indirect(pos1_sb[:]), picked["key2", t][:], ALU.subtract
            )
            terms[t] = [picked["lead", t]]

        def key_both(t):
            key_plain(t, pos1_sb, "key1")
            key_plain(t, pos2_sb, "key2", -1.0)
            terms[t] = [picked["key1", t], picked["key2", t]]

        def turn_leads(t0):
            lead_bank[t0] = psum.tile([P, 2, 2, P], F32, name="lead_bank%d" % t0, tag="bank%d" % BANK["lead%d" % t0])
            for u in (1, 0):
                for c in range(2):
                    for n, term in enumerate(terms[t0 + u]):
                        nc.tensor.matmul(
                            lead_bank[t0][:, c, u, :],
                            lhsT=term[:, c * P : (c + 1) * P],
                            rhs=ident[:],
                            is_transpose=True,
                            start=(n == 0),
                            stop=(n == len(terms[t0 + u]) - 1),
                        )

        def shares(t0):
            share_rows[t0] = fresh([P, 2, 2, P], F32, "share_rows%d" % t0)
            for c in range(2):
                nc.scalar.activation(
                    share_rows[t0][:, c, :, :], lead_bank[t0][:, c, :, :], ACT.Sigmoid, bias=bias[:, c : c + 1]
                )

        def turn_back(t0):
            share_bank[t0] = psum.tile([P, 2, V], F32, name="share_bank%d" % t0, tag="bank%d" % BANK["share%d" % t0])
            for u in range(2):
                for c in range(2):
                    nc.tensor.transpose(share_bank[t0][:, u, c * P : (c + 1) * P], share_rows[t0][:, c, u, :], ident[:])

        def value_second(t, engine=nc.scalar):
            if engine is nc.scalar:
                nc.scalar.activation(pair(second, t, "second"), res[1, t][:].indirect(pos2_sb[:]), ACT.Copy)
            else:
                nc.vector.tensor_copy(pair(second, t, "second"), res[1, t][:].indirect(pos2_sb[:]))

        def value_gap(t):
            nc.vector.tensor_tensor(
                pair(gap, t, "gap"), res[1, t][:].indirect(pos1_sb[:]), pair(second, t, "second"), ALU.subtract
            )

        def value_step(t0):
            step[t0] = fresh([P, 2, V], F32, "step%d" % t0)
            nc.vector.tensor_tensor(step[t0][:], gap[t0][:], share_bank[t0][:], ALU.mult)

        def value_mean(t0):
            mean[t0] = fresh([P, 2, V], F32, "mean%d" % t0)
            nc.vector.tensor_tensor(mean[t0][:], step[t0][:], second[t0][:], ALU.add)

        result = keep.tile([P, PACK, V], F32, name="result")
        out_rows = out_0.rearrange("(p t) v -> p t v", t=PACK)

        def gate_on_scalar(t):
            nc.scalar.activation(pair(gate, t, "gate"), res[2, t][:].indirect(own_sb[:]), ACT.Sigmoid)

        def finish_pair(t0):
            nc.vector.tensor_tensor(result[:, t0 : t0 + 2, :], gate[t0][:], mean[t0][:], ALU.mult)

        def finish_gated(t):
            nc.vector.tensor_tensor(result[:, t, :], pair(gate, t, "gate"), pair(mean, t, "mean"), ALU.mult)

        def finish(t, v0=0, v1=V):
            nc.vector.tensor_tensor(
                result[:, t, v0:v1],
                res[2, t][:].indirect(own_sb[:, v0 // 16 : v1 // 16]),
                pair(mean, t, "mean")[:, v0:v1],
                ALU.mult,
            )

        def store(t0, t1):
            nc.sync.dma_start(out_rows[:, t0:t1, :], result[:, t0:t1, :])

        def key_on_vector(t):
            picked["key1", t] = fresh([P, V], F32, "key1%d" % t)
            nc.vector.tensor_copy(picked["key1", t][:], res[0, t][:].indirect(pos1_sb[:]))

        round_weight(1, 0, nc.gpsimd, 0, 64)
        round_weight(1, 0, nc.gpsimd, 64, P)
        for n in range(2):
            nc.vector.tensor_copy(res[0, 1][:, halves[n]], half_banks[1, n][:])
        for g in range(PASSES):
            one_pass(0, g, 3)
        for t in range(2):
            key_plain(t, pos2_sb, "key2", -1.0)
            key_on_vector(t)
        leave_bank(0, 3)
        leave_bank(0, 2, nc.vector)
        for t in (3, 2):
            key_plain(t, pos2_sb, "key2", -1.0)
            key_plain(t, pos1_sb, "key1")
        for t in range(PACK):
            terms[t] = [picked["key1", t], picked["key2", t]]
        turn_leads(0)
        quantize_weight(1, 0)
        multiply(1, 0)
        prepare(1, 1)
        multiply(1, 1)
        prepare(2, 0)
        shares(0)
        leave_bank(1, 0)
        leave_bank(1, 1)
        turn_leads(2)
        turn_back(0)
        value_second(0)
        value_second(1)
        multiply(2, 0)
        shares(2)
        turn_back(2)
        round_half(2, 1, 0)
        round_half(2, 1, 1)
        quantize_half(2, 1, 0)
        value_gap(0)
        value_gap(1)
        quantize_half(2, 1, 1)
        multiply(2, 1)
        leave_bank(1, 2)
        leave_bank(1, 3)
        value_second(2)
        value_second(3)
        value_step(0)
        value_gap(2)
        value_gap(3)
        value_mean(0)
        value_step(2)
        leave_bank(2, 0, func=ACT.Sigmoid)
        leave_bank(2, 1, func=ACT.Sigmoid)
        leave_bank(2, 2)
        leave_bank(2, 3)
        gate_on_scalar(2)
        gate_on_scalar(3)
        finish(0)
        store(0, 1)
        value_mean(2)
        finish(1)
        store(1, 2)
        finish_gated(2)
        store(2, 3)
        pieces = (slice(0, 96), slice(96, 176), slice(176, V))
        for cols in pieces:
            nc.vector.tensor_tensor(result[:, 3, cols], gate[2][:, 1, cols], mean[2][:, 1, cols], ALU.mult)
        store(3, 4)

        out_grouped = keep.tile([P, V * PACK], BF16, name="out_grouped", align_bytes=64)
        dst = out_grouped[:].rearrange("p (c i t) -> p c t i", i=4, t=PACK)
        src = result[:].rearrange("p t (c i) -> p c t i", i=4)
        for n, cols in enumerate(pieces):
            runs = slice(cols.start // 4, cols.stop // 4)
            if n == 0:
                nc.scalar.copy(dst[:, runs], src[:, runs])
            else:
                nc.vector.tensor_copy(dst[:, runs], src[:, runs])
        out_codes = keep.tile([P, V], U32, name="out_codes", align_bytes=64)
        out_scales = keep.tile([P, V], U8, name="out_scales", align_bytes=64)
        nc.vector.quantize_mx(out=out_codes[:].bitcast(FP8X4), scales=out_scales[:], in_=out_grouped[:])
        nc.sync.dma_start(out_1[0].rearrange("p n t -> p (n t)").bitcast(I32), out_codes[:].bitcast(I32))
        for q in range(QUADS):
            queue = nc.scalar if q % 2 == 0 else nc.sync
            queue.dma_start(
                out_2[0, ROWS * q : ROWS * (q + 1), :].bitcast(I32),
                out_scales[32 * q : 32 * q + ROWS, :].bitcast(I32),
            )
